import numpy as np, ml_dtypes
CORES = [16,18,20,22]
N = 4
BF = ml_dtypes.bfloat16
def gentries(a):
    return np.ascontiguousarray(a.reshape(8, 16, -1).transpose(0, 2, 1)).reshape(8, -1)
def gtable(e):
    e = np.asarray(e); return np.ascontiguousarray(e.reshape(8, -1, 16).transpose(0, 2, 1)).reshape(128, -1).astype(np.int32)
P, S, H, C, D, TH = 2048, 256, 4096, 4, 3, 11008
W = P + (N - 1) * S
def stored(v):
    return np.stack([gtable(np.reshape(v[r], (8, -1))) for r in range(N)])
def setup_inputs(rng):
    v = rng.integers(0, 8, (N, 8, 16, P)) + rng.integers(32, 128, (N, 8, 1, P)) * (np.arange(16)[:, None] == rng.integers(0, 16, (N, 8, 1, P)))
    return {"x": v.reshape(N, 128, P).astype(np.float32).astype(BF), "sus": np.floor(256 * rng.random((N, 128, H)) ** 2).astype(np.float32).astype(BF),
            "hist": stored(rng.integers(0, H, (N, 8, P))), "home": stored(rng.integers(0, W, (N, 8, C, P))), "away": stored(rng.integers(0, W, (N, 8, C, P))),
            "shown": stored(rng.integers(0, P, (N, 8, N - 1, S)))}
def setup_inputs_ties(rng):
    d = setup_inputs(rng); b = TH // 64
    d["x"] = (64 * (rng.random((N, 128, P)) * C < 0.25)).astype(np.float32).astype(BF)
    d["sus"] = rng.choice(np.array([0, 0, b, b + 1]), (N, 128, H)).astype(np.float32).astype(BF); return d
def setup_inputs_ends(rng):
    d = setup_inputs(rng); e = np.array([0, P - 1] + [P + k * S for k in range(N - 1)] + [P + k * S + S - 1 for k in range(N - 1)])
    for a, w in (("home", e), ("away", e), ("shown", e[:2]), ("hist", np.array([0, 15, H - 16, H - 1]))):
        d[a] = np.where(rng.random(d[a].shape) < 0.5, rng.choice(w, d[a].shape), d[a]).astype(np.int32)
    return d
def setup_inputs_one(rng):
    d = setup_inputs(rng); o = np.ones((1, 1, P), np.int64)
    d["hist"] = stored(rng.integers(0, H, (N, 8, 1)) * o); d["home"] = stored(rng.integers(0, W, (N, 8, 1)) * np.ones((1, 1, C * P), np.int64)); return d
def setup_inputs_far(rng):
    d = setup_inputs(rng); own = rng.integers(0, P, (N, 8, C, P)); out = rng.integers(P, W, (N, 8, C, P)); even = (np.arange(N) % 2 == 0)[:, None, None, None]
    d["home"] = stored(np.where(even, out, own)); d["away"] = stored(np.where(even, own, out)); return d
def setup_inputs_spread(rng):
    d = setup_inputs(rng); s = np.where(rng.random((N, 8, 1, P)) < 0.5, rng.integers(0, 4, (N, 8, 1, P)), rng.integers(0, 9, (N, 8, 1, P)))
    d["x"] = np.floor(256 * rng.random((N, 8, 16, P)) * np.exp2(-s)).reshape(N, 128, P).astype(np.float32).astype(BF)
    d["sus"] = np.floor(256 * rng.random((N, 8, 16, H)) * np.exp2(-rng.integers(0, 6, (N, 8, 1, H)))).reshape(N, 128, H).astype(np.float32).astype(BF)
    for a, n, k in (("hist", H, P), ("home", W, C * P), ("away", W, C * P), ("shown", P, (N - 1) * S)):
        d[a] = stored((np.floor(n * rng.random((N, 8, k)) ** 3).astype(np.int64) + rng.integers(0, n, (N, 8, 1))) % n)
    return d
def check_inputs(d):
    bad = []
    for a in ("x", "sus"):
        v = d[a].astype(np.float32)
        if not ((v >= 0) & (v <= 255) & (v == np.floor(v))).all(): bad.append(a)
    for a, n in (("hist", H), ("home", W), ("away", W), ("shown", P)):
        if not ((d[a] >= 0) & (d[a] < n)).all(): bad.append(a)
    return bad
def reference(x, sus, hist, home, away, shown):
    load = x.astype(np.float32).astype(np.int64).reshape(N, 8, 16, P); tab = sus.astype(np.float32).astype(np.int64).reshape(N, 8, 16, H)
    code = np.stack([gentries(hist[r]) for r in range(N)]).astype(np.int64); ill = np.zeros((N, 8, P), bool)
    near = np.stack([gentries(home[r]) for r in range(N)]).reshape(N, 8, C, P); far = np.stack([gentries(away[r]) for r in range(N)]).reshape(N, 8, C, P)
    give = np.stack([gentries(shown[r]) for r in range(N)]).reshape(N, 8, N - 1, S)
    for day in range(D):
        new = load >> 1
        for r in range(N):
            parts = [load[r]]
            for q in range(N):
                if q != r: parts.append(np.take_along_axis(load[q], give[q][:, None, r if r < q else r - 1], 2))
            win = np.concatenate(parts, 2)
            con = np.where(ill[r][:, None], far[r], near[r]).reshape(8, 1, C * P)
            pressure = np.sum(np.take_along_axis(win, con, 2).reshape(8, 16, C, P), axis=2)
            score = pressure * np.take_along_axis(tab[r], code[r][:, None], 2)
            best = np.argmax(score, axis=1); hit = np.max(score, axis=1) > TH
            new[r] += 64 * ((np.arange(16)[:, None] == best[:, None]) & hit[:, None])
            code[r] = np.where(hit, (16 * code[r] + best) & (H - 1), code[r]); ill[r] = hit
        load = new
    return {"y": load.reshape(N, 128, P).astype(np.float32), "h": stored(code).astype(np.float32)}

@@ -1,0 +1,469 @@
+from concourse.bass import DstId, RemoteDMATransfer
+from concourse.mybir import AluOpType, ActivationFunctionType
+
+P, S, W, H, TH, DAYS = 2048, 256, 2816, 4096, 11008, 3
+N, U = 512, 4
+GROUPS = [(0, 2), (2, 3), (3, 4)]
+BATCHES = [(0, 4)]
+PAIRED = {(3, 0), (3, 1), (3, 2), (3, 3)}
+TWO = ["xx", "uu"]
+
+SCRATCH = {
+    "win1": ("sbuf", [128, W], "bfloat16"), "win2": ("sbuf", [128, W], "bfloat16"), "win3": ("sbuf", [128, W], "bfloat16"),
+    "tab": ("sbuf", [128, H], "bfloat16"),
+    "shown_i": ("sbuf", [128, 48], "int32"), "shown_u": ("sbuf", [128, 48], "uint16"),
+    "c1": ("sbuf", [128, 128], "int32"), "c2": ("sbuf", [128, 128], "int32"), "c3": ("sbuf", [128, 128], "int32"),
+    "c4": ("sbuf", [128, 128], "float32"),
+    "hu1": ("sbuf", [128, 128], "uint16"), "hu2": ("sbuf", [128, 128], "uint16"), "hu3": ("sbuf", [128, 128], "uint16"),
+    "home_i": ("sbuf", [128, 512], "int32"), "away_i": ("sbuf", [128, 512], "int32"), "dif": ("sbuf", [128, 512], "float32"),
+    "cu1": ("sbuf", [128, 512], "uint16"), "cu2": ("sbuf", [128, 512], "uint16"), "cu3": ("sbuf", [128, 512], "uint16"),
+    "lowc": ("sbuf", [128, 128], "int32"), "lowx": ("sbuf", [128, 128], "float32"), "ac": ("sbuf", [128, 128], "float32"),
+    "t1": ("sbuf", [128, 128], "float32"), "t2": ("sbuf", [128, 128], "float32"),
+    "hd": ("sbuf", [128, 512], "float32"), "mg": ("sbuf", [128, 512], "float32"),
+    "gc": ("sbuf", [128, 4 * P], "bfloat16"), "gs": ("sbuf", [128, P], "bfloat16"),
+    "g0": ("sbuf", [128, P], "float32"), "g2": ("sbuf", [128, P], "float16"),
+    "st0": ("sbuf", [128, P], "bfloat16"), "st1": ("sbuf", [128, P], "bfloat16"),
+    "sc": ("sbuf", [128, P], "float32"), "fs": ("sbuf", [128, P], "float32"),
+    "zi": ("sbuf", [128, 32 * U], "int32"), "zz": ("sbuf", [128, 32 * U], "int32"),
+    "feat": ("sbuf", [128, 96 * U], "bfloat16"), "tts": ("sbuf", [128, 128 * U], "bfloat16"),
+    "h1": ("sbuf", [128, P], "bfloat16"), "h2": ("sbuf", [128, P], "bfloat16"), "h3": ("sbuf", [128, P], "bfloat16"),
+    "hr": ("sbuf", [128, P], "bfloat16"),
+    "snd1": ("sbuf", [128, 3 * S], "bfloat16"), "snd2": ("sbuf", [128, 3 * S], "bfloat16"), "snd3": ("sbuf", [128, 3 * S], "bfloat16"),
+    "yo": ("sbuf", [128, P], "float32"),
+    "ones": ("sbuf", [128, 128], "bfloat16"), "neg32": ("sbuf", [128, 128], "bfloat16"),
+    "ri": ("sbuf", [128, 128], "bfloat16"), "rih": ("sbuf", [128, 128], "float16"),
+    "ris": ("sbuf", [128, 128], "bfloat16"), "idn": ("sbuf", [128, 128], "bfloat16"),
+    "ev": ("sbuf", [128, 512], "bfloat16"), "em": ("sbuf", [128, 512], "bfloat16"),
+    "mz": ("sbuf", [128, 128], "bfloat16"), "lm": ("sbuf", [128, 512], "bfloat16"),
+    "s1f": ("sbuf", [128, 16], "float32"), "s1q": ("sbuf", [128, 16], "float32"),
+    "d0": ("sbuf", [128, 1024], "float32"),
+    "pp": ("psum", [128, 1024], "float32"), "xx": ("psum", [128, 1024], "float32"), "uu": ("psum", [128, 1024], "float32"),
+    "tl": ("psum", [128, 512], "float32"), "hp": ("psum", [128, 512], "float32"),
+}
+BANKS = [n for n in SCRATCH if SCRATCH[n][0] == "psum"]
+DMAS = ["x", "shown", "hist", "sus", "home", "away", "h"] + ["y%d" % u for u in range(U)]
+SEMAPHORES = ["q" + q for q in "VSPG"] + ["d_" + n for n in DMAS] + ["arr1", "arr2", "arr3", "sent"]
+
+
+def routes(T, topo, core):
+    peers = [c for c in T.cores if c != core]
+    peers = [c for c in peers if topo.die(c) == topo.die(core)] + [c for c in peers if topo.die(c) != topo.die(core)]
+    e = topo.engines(core, peers[0])
+    return [[(peers[0], e[0::2]), (peers[1], e[1::2])], [(peers[2], topo.engines(core, peers[2]))]]
+
+
+def part(a, b):
+    return b if b < a else b - 1
+
+
+def build_graph():
+    ops, seen = [], {}
+    A, F = AluOpType, ActivationFunctionType
+
+    def op(cost, emit, rd=(), wr=(), lat=None, token=None, group=None, deps=()):
+        i, dep = len(ops), set(deps)
+        acc = [(r, False) for r in rd] + [(r, True) for r in wr]
+        acc = [((b, lo // 512 * 512, -(-hi // 512) * 512), True) if b in BANKS else ((b, lo, hi), w) for (b, lo, hi), w in acc]
+        for (b, lo, hi), w in acc:
+            for l2, h2, j, w2, g2 in seen.get(b, ()):
+                if l2 < hi and lo < h2 and (w or w2) and j != i and (group is None or g2 != group):
+                    dep.add(j)
+        for (b, lo, hi), w in acc:
+            old = seen.setdefault(b, [])
+            if w and group is None:
+                old[:] = [t for t in old if not (lo <= t[0] and t[1] <= hi)]
+            old.append((lo, hi, i, w, group))
+        ops.append({"cost": cost, "emit": emit, "deps": sorted(dep), "lat": lat, "token": token})
+        return i
+
+    def v(n, c=1.0): return {"V": (1, max(64, n * c), 0, 0)}
+    def vs(n, c=1.0): return {"V": (1, n * c, 0, 0), "S": (1, n, 0, 0)}
+    def gat(n): return {"V": (1, 0, n, 0), "S": (1, 0, n, 0)}
+    def pe(k, n): return {"P": (k, 0, 0, k * max(64, n))}
+    def gp(n): return {"G": (2, 2 * n, 0, 0)}
+
+    def load(name, dst, lo, hi, q, kb):
+        op({q: (1, 0, 0, 0)}, lambda x, q: [x["eng"][q].dma_start(x["T"][dst][:, lo:hi], x["T"][name][:])], wr=[(dst, lo, hi)], lat=("dma", kb), token=name)
+
+    load("shown", "shown_i", 0, 48, "S", 24)
+    load("x", "win1", 0, P, "Y", 512)
+    load("hist", "c1", 0, 128, "S", 64)
+    load("sus", "tab", 0, H, "Y", 1600)
+    load("home", "home_i", 0, 512, "S", 800)
+    load("away", "away_i", 0, 512, "Y", 2100)
+
+    def fill(buf, rows, lo, hi, val, key=None, step=1):
+        op(v((hi - lo) // step), lambda x, q: [x["v"].memset(x["T"][buf][rows[0]:rows[1], lo:hi:step], val)], wr=[(key or buf, 0 if step > 1 else lo, hi)])
+
+    def select(buf, src, rows, lo, hi, slo, shi, pattern, base, cm, rkey, wkey):
+        op(gp(hi - lo), lambda x, q: [x["g"].affine_select(x["T"][buf][rows[0]:rows[1], lo:hi], x["T"][src][rows[0]:rows[1], slo:shi], pattern, A.is_equal, 0.0, base, cm)],
+           rd=[(rkey, slo, shi)], wr=[(wkey, lo, hi)])
+
+    def iota(buf, rows, n, pattern, base, key):
+        op(gp(n), lambda x, q: [x["g"].iota(x["T"][buf][rows[0]:rows[1], 0:n], pattern, base, 0, allow_small_or_imprecise_dtypes=True)], wr=[(key, 0, n)])
+
+    full = (0, 128)
+    fill("ones", full, 0, 128, 1.0)
+    fill("neg32", full, 0, 128, -32.0)
+    select("idn", "ones", full, 0, 128, 0, 128, [[-1, 128]], 0, 1, "ones", "idn")
+    select("ri", "ones", full, 0, 128, 0, 128, [[-16, 8], [1, 16]], -15, 1, "ones", "ri")
+    select("ris", "neg32", full, 0, 128, 0, 128, [[-16, 8], [1, 16]], -15, 1, "neg32", "ris")
+    op(v(128), lambda x, q: [x["v"].tensor_copy(x["T"].rih[:], x["T"].ri[:])], rd=[("ri", 0, 128)], wr=[("rih", 0, 128)])
+    fill("d0", full, 0, 1024, 1.0)
+    fill("d0", full, 0, 1024, 16777216.0, step=16)
+    fill("feat", full, 64, 96 * U, 1.0, step=96, key="one")
+    iota("s1f", (64, 96), 16, [[1, 16]], 1, "s1f")
+    iota("ev", (0, 32), 512, [[0, 32], [128, 16]], 128, "ev0")
+    fill("ev", (32, 64), 0, 512, -64.0, key="ev1")
+    op(v(16), lambda x, q: [x["v"].tensor_tensor(x["T"].s1q[64:96, :], x["T"].s1f[64:96, :], x["T"].s1f[64:96, :], A.mult)], rd=[("s1f", 0, 16)], wr=[("s1q", 0, 16)])
+    op(v(16), lambda x, q: [x["v"].tensor_scalar(x["T"].em[64:96, 0:16], x["T"].s1q[64:96, :], -64.0, 64.0, A.mult, A.add)], rd=[("s1q", 0, 16)], wr=[("em2", 0, 16)])
+    for w in (16, 32, 64, 128, 256):
+        op(v(w), lambda x, q, w=w: [x["v"].tensor_copy(x["T"].em[64:96, w:2 * w], x["T"].em[64:96, 0:w])], rd=[("em2", 0, w)], wr=[("em2", w, 2 * w)])
+    for f in range(2):
+        select("em", "ev", (32 * f, 32 * f + 32), 0, 512, 0, 512, [[-8, 4], [-1, 8], [0, 16]], 0, 1, "ev%d" % f, "em%d" % f)
+    EM = [("em0", 0, 512), ("em1", 0, 512), ("em2", 0, 512)]
+    select("mz", "ones", (0, 32), 0, 128, 0, 128, [[-1, 8], [0, 4], [-8, 4]], 0, 1, "ones", "mz")
+    for h in range(4):
+        select("lm", "mz", (0, 32), 128 * h, 128 * h + 128, 0, 128, [[0, 8], [1, 4], [0, 4]], -h, 0, "mz", "lm")
+
+    def copy(dst, src, lo, hi):
+        op(v(hi - lo), lambda x, q: [x["v"].tensor_copy(x["T"][dst][:, lo:hi], x["T"][src][:, lo:hi])], rd=[(src, lo, hi)], wr=[(dst, lo, hi)])
+
+    def gather(dst, lo, hi, win, whi, lst, llo, bias, lkey=None):
+        k = (hi - lo) // 16
+
+        def emit(x, q):
+            T = x["T"]
+            a = llo if lkey is None else llo(x)
+            o, w = T[dst][:, lo:hi], T[win][:, 0:whi].indirect(T[lst][:, a:a + k])
+            if q == "S":
+                return [x["s"].activation(o, w, F.Identity, bias=bias)] if bias else [x["s"].activation(o, w, F.Copy)]
+            return [x["v"].tensor_scalar(o, w, bias, None, A.add)] if bias else [x["v"].tensor_copy(o, w)]
+        lr = (lst, llo, llo + k) if lkey is None else (lst,) + lkey
+        return op(gat(hi - lo), emit, rd=[(win, 0, whi), lr], wr=[(dst, lo, hi)])
+
+    def send(d):
+        win, snd, arr = "win%d" % d, "snd%d" % d, "arr%d" % d
+        for i in range(3):
+            def llo(x, i=i):
+                to = [t for call in x["routes"] for t in call][i][0]
+                return 16 * part(x["rank"], x["T"].rank_of(to))
+            gather(snd, S * i, S * i + S, win, P, "shown_u", llo, 0.0, lkey=(0, 48))
+        calls, pos = [], 0
+        for n, size in enumerate((2, 1)):
+            def emit(x, q, n=n, pos=pos):
+                T, trs = x["T"], []
+                for j, (to, eng) in enumerate(x["routes"][n]):
+                    rid, pid, _ = x["topo"].addr(to)
+                    at = P + S * part(T.rank_of(to), x["rank"])
+                    trs.append((rid, pid, T[win][:, at:at + S], T[snd][:, S * (pos + j):S * (pos + j) + S], sum(1 << e for e in eng)))
+                    x["sent"][0] += len(eng)
+                if len(trs) == 1:
+                    rid, pid, o, a, m = trs[0]
+                    x["g"].remote_dma(o, a, T.sem[arr], T.sem["sent"], pid, rid, m)
+                else:
+                    x["g"].remote_dma_fused([RemoteDMATransfer(dst_ids=[DstId(rid=r, pnc=p)], dma_engine_mask=m, remote_sem=T.sem[arr], srcs=[a], dsts=[o])
+                                             for r, p, o, a, m in trs], local_sem=T.sem["sent"])
+                return []
+            calls.append(op({"G": (12, 0, 0, 0)}, emit, rd=[(snd, S * pos, S * (pos + size))], lat=("remote", 64 * size), token="sent"))
+            pos += size
+        return op({"-": (0, 0, 0, 0)}, None, wr=[(win, P, W)], token=arr, deps=calls)
+
+    def tables(d, u):
+        i0, e, st, b, uu = N * u, N * u + N, "st%d" % (d % 2), N * (u % 2), TWO[u // 2]
+        gather("gs", i0, e, "tab", H, "hu%d" % d, i0 // 16, 0.0)
+        op(pe(4, 128), lambda x, q: [x["t"].matmul(x["T"][uu][:, b + 128 * k:b + 128 * k + 128], x["T"].gs[:, i0 + k:e:4], x["T"].ris[:], True, True) for k in range(4)],
+           rd=[("gs", i0, e), ("ris", 0, 128)], wr=[(uu, b, b + N)])
+
+        def out(x, q):
+            o, w = x["T"][st][:, i0:e], x["T"][uu][:, b:b + N]
+            return [x["s"].activation(o, w, F.Copy)] if q == "S" else [x["v"].tensor_copy(o, w)]
+        op(vs(N), out, rd=[(uu, b, b + N)], wr=[(st, i0, e)])
+
+    def halves(d, u):
+        i0, e, dst, win = N * u, N * u + N, "h%d" % d, "win%d" % d
+        to = dst if d < DAYS else "hr"
+        add = -255.375 if d == 1 else -127.875
+
+        def emit(x, q):
+            o, w = x["T"][to][:, i0:e], x["T"][win][:, i0:e]
+            return [x["s"].activation(o, w, F.Identity, bias=add, scale=0.5)] if q == "S" else [x["v"].tensor_scalar(o, w, 0.5, add, A.mult, A.add)]
+        op(vs(N, 0.5), emit, rd=[(win, i0, e)], wr=[(to, i0, e)])
+        if d == DAYS:
+            def back(x, q):
+                o, w = x["T"][dst][:, i0:e], x["T"].hr[:, i0:e]
+                return [x["s"].activation(o, w, F.Identity, bias=255.0)] if q == "S" else [x["v"].tensor_scalar(o, w, 255.0, None, A.add)]
+            op(vs(N, 0.5), back, rd=[("hr", i0, e)], wr=[(dst, i0, e)])
+
+    def base(d, u):
+        i0, e, hh, uu, b = N * u, N * u + N, "h%d" % d, TWO[u // 2], N * (u % 2)
+        op(pe(1, N), lambda x, q: [x["t"].matmul(x["T"][uu][:, b:b + N], x["T"].idn[:], x["T"][hh][:, i0:e], True, False)],
+           rd=[(hh, i0, e), ("idn", 0, 128)], wr=[(uu, b, b + N)])
+
+    def low(d):
+        c = "c%d" % d
+        op(v(128), lambda x, q: [x["v"].tensor_scalar(x["T"].lowc[:], x["T"][c][:], 255, None, A.bitwise_and)], rd=[(c, 0, 128)], wr=[("lowc", 0, 128)])
+        op(v(128), lambda x, q: [x["v"].tensor_scalar(x["T"].lowx[:], x["T"].lowc[:], 16.0, -1.0, A.mult, A.add)], rd=[("lowc", 0, 128)], wr=[("lowx", 0, 128)])
+        op(v(128, 2), lambda x, q: [x["v"].tensor_tensor(x["T"].ac[:], x["T"].lowx[:], x["T"][c][:], A.subtract)], rd=[("lowx", 0, 128), (c, 0, 128)], wr=[("ac", 0, 128)])
+
+    def pressure(d, u):
+        i0, e, b, win, cu = N * u, N * u + N, N * (u % 2), "win%d" % d, "cu%d" % d
+        bias = 0.0 if d == 1 else 255.0
+        pieces = []
+        mine = [c for c in range(4) if (c, u) in PAIRED]
+        for c in range(4):
+            a = 128 * c + i0 // 16
+            if mine and c == 0:
+                gather("g0", i0, e, win, W, cu, a, 2 * bias)
+                pieces.append(("g2", 0, "rih"))
+            elif c in mine:
+                op({"V": (1, 0, N, 0)},
+                   lambda x, q, a=a: [x["v"].tensor_tensor(x["T"].g2[:, i0:e], x["T"][win][:, 0:W].indirect(x["T"][cu][:, a:a + N // 16]), x["T"].g0[:, i0:e], A.add)],
+                   rd=[(win, 0, W), (cu, a, a + N // 16), ("g0", i0, e)], wr=[("g2", i0, e)])
+            else:
+                gather("gc", P * c + i0, P * c + e, win, W, cu, a, bias)
+                pieces.append(("gc", P * c, "ri"))
+        last = len(pieces) - 1
+        for buf, at, idn in pieces:
+            def emit(x, q, buf=buf, at=at + i0, idn=idn):
+                T, key = x["T"], (d, u)
+                t = x["open"].get(key, 0)
+                x["open"][key] = t + 1
+                return [x["t"].matmul(T.pp[:, b + 128 * k:b + 128 * k + 128], T[buf][:, at + k:at + N:4], T[idn][:], t == 0 and k == 0, t == last and k == 3) for k in range(4)]
+            op(pe(4, 128), emit, rd=[(buf, at + i0, at + e), (idn, 0, 128)], wr=[("pp", b, b + N)], group=(d, u))
+
+    def outcome(d, u0, u1):
+        i0, e, n, m0, m1 = N * u0, N * u1, N * (u1 - u0), 32 * u0, 32 * u1
+        st, hh, k, uu, b = "st%d" % (d % 2), "h%d" % d, u1 - u0, TWO[u0 // 2], N * (u0 % 2)
+        op(v(n), lambda x, q: [x["v"].tensor_tensor(x["T"].sc[:, i0:e], x["T"].pp[:, b:b + n], x["T"][st][:, i0:e], A.mult)], rd=[("pp", b, b + n), (st, i0, e)], wr=[("sc", i0, e)])
+        op(v(n), lambda x, q: [x["v"].tensor_tensor_scan(x["T"].fs[:, i0:e], x["T"].d0[:, 0:n], x["T"].sc[:, i0:e], 0.0, A.add, A.min)], rd=[("sc", i0, e), ("d0", 0, 1024)], wr=[("fs", i0, e)])
+        op(v(32 * k), lambda x, q: [x["v"].tensor_scalar(x["T"].zi[:, m0:m1], x["T"].fs[:, i0 + 15:e:16], 1.0, -32.0 * TH, A.add, A.min)], rd=[("fs", i0, e)], wr=[("zi", m0, m1)])
+        op(v(32 * k), lambda x, q: [x["v"].tensor_scalar(x["T"].zz[:, m0:m1], x["T"].zi[:, m0:m1], 31, None, A.bitwise_and)], rd=[("zi", m0, m1)], wr=[("zz", m0, m1)])
+        for u in range(u0, u1):
+            a, f, j = 32 * u, 96 * u, 128 * (u - u0)
+            op(v(32), lambda x, q, a=a, f=f: [x["v"].tensor_copy(x["T"].feat[:, f:f + 32], x["T"].zz[:, a:a + 32])], rd=[("zz", a, a + 32)], wr=[("feat", f, f + 32)])
+            op(v(32, 2), lambda x, q, a=a, f=f: [x["v"].tensor_tensor(x["T"].feat[:, f + 32:f + 64], x["T"].zz[:, a:a + 32], x["T"].zz[:, a:a + 32], A.mult)],
+               rd=[("zz", a, a + 32)], wr=[("feat", f + 32, f + 64)])
+            op(pe(1, 128), lambda x, q, f=f, j=j: [x["t"].matmul(x["T"].tl[0:65, j:j + 128], x["T"].feat[:, f:f + 65], x["T"].idn[:], True, True)],
+               rd=[("feat", f, f + 65), ("one", 0, 96 * U), ("idn", 0, 128)], wr=[("tl", 0, 512)])
+
+        def down(x, q):
+            o, w = x["T"].tts[0:65, 128 * u0:128 * u1], x["T"].tl[0:65, 0:128 * k]
+            return [x["s"].activation(o, w, F.Copy)] if q == "S" else [x["v"].tensor_copy(o, w)]
+        op(vs(128 * k), down, rd=[("tl", 0, 512)], wr=[("tts", 128 * u0, 128 * u1)])
+        for u in range(u0, u1):
+            j, t = N * (u % 2), 128 * u
+            op(pe(4, 128), lambda x, q, j=j, t=t: [x["t"].matmul(x["T"][uu][:, j + r:j + N:4], x["T"].em[0:65, 128 * r:128 * r + 128], x["T"].tts[0:65, t:t + 128], False, r == 3)
+                                                   for r in range(4)], rd=[("tts", t, t + 128)] + EM, wr=[(uu, j, j + N)])
+        to = "win%d" % (d + 1) if d < DAYS else "yo"
+        op(v(n), lambda x, q: [x["v"].tensor_tensor(x["T"][to][:, i0:e], x["T"][uu][:, b:b + n], x["T"][hh][:, i0:e], A.max)], rd=[(uu, b, b + n), (hh, i0, e)], wr=[(to, i0, e)])
+        if d == DAYS:
+            op({"Y": (1, 0, 0, 0)}, lambda x, q: [x["y"].dma_start(x["T"].y[:, i0:e], x["T"].yo[:, i0:e])], rd=[("yo", i0, e)], lat=("dma", 256 * k), token="y%d" % u0)
+
+    def histories(d, u0, u1):
+        lo, hi, k = 32 * u0, 32 * u1, 32 * (u1 - u0)
+        z0, h0 = 256, 384
+        op(pe(4, k), lambda x, q: [x["t"].matmul(x["T"].tl[:, z0 + lo:z0 + hi], x["T"].lm[0:32, 128 * h:128 * h + 128], x["T"].tts[0:32, 128 * u0 + h:128 * u1:4], h == 0, h == 3)
+                                   for h in range(4)], rd=[("tts", 128 * u0, 128 * u1), ("lm", 0, 512)], wr=[("tl", 0, 512)])
+        c, cn, hu = "c%d" % d, "c%d" % (d + 1), "hu%d" % (d + 1)
+        op(v(k), lambda x, q: [x["v"].tensor_scalar(x["T"].tl[:, h0 + lo:h0 + hi], x["T"].tl[:, z0 + lo:z0 + hi], 1.0, None, A.min)], wr=[("tl", 0, 512)])
+        op(v(k), lambda x, q: [x["v"].tensor_tensor(x["T"].t1[:, lo:hi], x["T"].tl[:, h0 + lo:h0 + hi], x["T"].ac[:, lo:hi], A.mult)], rd=[("tl", 0, 512), ("ac", lo, hi)], wr=[("t1", lo, hi)])
+        op(v(k), lambda x, q: [x["v"].tensor_tensor(x["T"].t2[:, lo:hi], x["T"].tl[:, z0 + lo:z0 + hi], x["T"].t1[:, lo:hi], A.add)], rd=[("tl", 0, 512), ("t1", lo, hi)], wr=[("t2", lo, hi)])
+        op(v(k, 2), lambda x, q: [x["v"].tensor_tensor(x["T"][cn][:, lo:hi], x["T"].t2[:, lo:hi], x["T"][c][:, lo:hi], A.add)], rd=[("t2", lo, hi), (c, lo, hi)], wr=[(cn, lo, hi)])
+        if d < DAYS:
+            copy(hu, cn, lo, hi)
+
+    def contacts(d):
+        for c in range(4):
+            lo, hi = 128 * c, 128 * c + 128
+            op(v(128), lambda x, q, lo=lo, hi=hi: [x["v"].tensor_tensor(x["T"].hd[:, lo:hi], x["T"].tl[:, 384:512], x["T"].dif[:, lo:hi], A.mult)],
+               rd=[("tl", 0, 512), ("dif", lo, hi)], wr=[("hd", lo, hi)])
+        op(v(512), lambda x, q: [x["v"].tensor_tensor(x["T"].mg[:], x["T"].hp[:], x["T"].hd[:], A.add)], rd=[("hp", 0, 512), ("hd", 0, 512)], wr=[("mg", 0, 512)])
+        copy("cu%d" % d, "mg", 0, 512)
+
+    copy("shown_u", "shown_i", 0, 48)
+    send(1)
+    copy("hu1", "c1", 0, 128)
+    for u in range(U):
+        tables(1, u)
+    copy("cu1", "home_i", 0, 512)
+    copy("hp", "home_i", 0, 512)
+    op(v(512), lambda x, q: [x["v"].tensor_tensor(x["T"].dif[:], x["T"].away_i[:], x["T"].hp[:], A.subtract)], rd=[("away_i", 0, 512), ("hp", 0, 512)], wr=[("dif", 0, 512)])
+    for d in range(1, DAYS + 1):
+        low(d)
+        for u in range(U):
+            halves(d, u)
+        for u in range(U):
+            base(d, u)
+        for u0, u1 in GROUPS:
+            for u in range(u0, u1):
+                pressure(d, u)
+            outcome(d, u0, u1)
+            for b0, b1 in BATCHES:
+                if b1 == u1:
+                    histories(d, b0, b1)
+                    if d < DAYS:
+                        for w in range(b0, b1):
+                            tables(d + 1, w)
+        if d < DAYS:
+            send(d + 1)
+            contacts(d + 1)
+    op({"Y": (1, 0, 0, 0)}, lambda x, q: [x["y"].dma_start(x["T"].h[:], x["T"].c4[:])], rd=[("c4", 0, 128)], lat=("dma", 64), token="h")
+    return ops
+
+
+NOMINAL = {"V": 0.06, "S": 0.10, "P": 0.03, "G": 0.09, "Y": 0.10, "-": 0.0, "cyc": 0.00083, "gat": 1.5 * 0.00083, "pe": 0.00072,
+           "hop": 0.10, "own": 0.06, "dma": 2.0, "kb": 0.005, "remote": 2.0, "rkb": 0.008}
+SETS = [{}, {"gat": 1.1 * 0.00083, "remote": 2.5}, {"gat": 2.0 * 0.00083}, {"hop": 0.2, "own": 0.1, "pe": 0.00083, "remote": 3.0}]
+TRIES = 3000
+PLAN = {}
+
+
+def dur(op, q, m):
+    f, cyc, gat, pe = op["cost"][q]
+    return f * m[q] + cyc * m["cyc"] + gat * m["gat"] + pe * m["pe"]
+
+
+def late(op, m):
+    if op["lat"] is None:
+        return 0.0
+    kind, kb = op["lat"]
+    return m["dma"] + kb * m["kb"] if kind == "dma" else m["remote"] + kb * m["rkb"]
+
+
+def schedule(ops, users, m, noise, on):
+    n = len(ops)
+    prio = [0.0] * n
+    for i in range(n - 1, -1, -1):
+        prio[i] = dur(ops[i], on[i], m) + late(ops[i], m) + max([prio[j] + m["hop"] for j in users[i]] or [0.0])
+    key = [prio[i] + noise[i] for i in range(n)]
+    left = [len(o["deps"]) for o in ops]
+    done, free = [None] * n, {q: 0.0 for q in "VSPGY-"}
+    avail = [i for i in range(n) if left[i] == 0]
+    ready, out = [None] * n, []
+    while avail:
+        best = None
+        for i in avail:
+            q = on[i]
+            if ready[i] is None:
+                ready[i] = max([done[d] + (m["own"] if on[d] == q else m["hop"]) for d in ops[i]["deps"]] or [0.0])
+            r = max(free[q], ready[i])
+            if best is None or r < best[0] - 1e-9 or (r < best[0] + 1e-9 and key[i] > key[best[1]]):
+                best = (r, i)
+        r, i = best
+        q = on[i]
+        t = r + dur(ops[i], q, m)
+        if q != "-":
+            free[q] = t
+        done[i] = t + late(ops[i], m)
+        out.append((r, i, q))
+        avail.remove(i)
+        for j in users[i]:
+            left[j] -= 1
+            if left[j] == 0:
+                avail.append(j)
+    return out
+
+
+def replay(ops, order, m):
+    done, queue, free, span = {}, {}, {q: 0.0 for q in "VSPGY-"}, 0.0
+    for _, i, q in order:
+        r = free[q] if q != "-" else 0.0
+        for d in ops[i]["deps"]:
+            t = done[d] + (m["own"] if queue[d] == q else m["hop"])
+            if t > r:
+                r = t
+        t = r + dur(ops[i], q, m)
+        if q != "-":
+            free[q] = t
+        done[i], queue[i] = t + late(ops[i], m), q
+        span = max(span, done[i])
+    return span
+
+
+def plan():
+    if PLAN:
+        return PLAN
+    ops = build_graph()
+    n, state = len(ops), [12345]
+    users = [[] for _ in range(n)]
+    for i, o in enumerate(ops):
+        for d in o["deps"]:
+            users[d].append(i)
+
+    def rnd(k):
+        state[0] = (1103515245 * state[0] + 12345) % 2147483648
+        return (state[0] >> 8) % k
+    sets = [dict(NOMINAL, **s) for s in SETS]
+
+    def judge(noise, on):
+        order = schedule(ops, users, sets[0], noise, on)
+        return sum(replay(ops, order, m) for m in sets) / len(sets), order
+    flex = [i for i in range(n) if len(ops[i]["cost"]) > 1]
+    on = ["S" if len(o["cost"]) > 1 else list(o["cost"])[0] for o in ops]
+    noise = [0.0] * n
+    best, order = judge(noise, on)
+    for _ in range(TRIES):
+        noise2, on2 = noise[:], on[:]
+        for _ in range(1 << rnd(4)):
+            if rnd(5) < 2:
+                i = flex[rnd(len(flex))]
+                on2[i] = "V" if on[i] == "S" else "S"
+            else:
+                noise2[rnd(n)] += (rnd(1001) + rnd(1001) + rnd(1001) - 1500) / 250.0
+        t, order2 = judge(noise2, on2)
+        if t <= best:
+            best, order, noise, on = t, order2, noise2, on2
+    PLAN["ops"], PLAN["order"], PLAN["time"] = ops, order, best
+    PLAN["at"] = {i: k for k, (_, i, _) in enumerate(order)}
+    return PLAN
+
+
+def rank_program(g, core, T, topo):
+    rank = T.rank_of(core)
+    if rank is None:
+        return
+    p = plan()
+    ops = p["ops"]
+    eng = {"V": g.vector, "S": g.scalar, "P": g.tensor, "G": g, "Y": g.sync}
+    x = {"g": g, "v": g.vector, "s": g.scalar, "t": g.tensor, "y": g.sync, "T": T, "topo": topo, "rank": rank, "eng": eng,
+         "routes": routes(T, topo, core), "open": {}, "sent": [0]}
+    landing = sum(len(e) for c in T.cores if c != core for call in routes(T, topo, c) for to, e in call if to == core)
+    count = {q: 0 for q in eng}
+    seen = {q: {} for q in eng}
+    tok, known, final = {}, {}, {}
+    for _, i, q in p["order"]:
+        o = ops[i]
+        if q == "-":
+            tok[i], known[i] = (o["token"], landing), {o["token"]: landing}
+            final[o["token"]] = landing
+            continue
+        for d in sorted(o["deps"], key=lambda d: -p["at"][d]):
+            s, n = tok[d]
+            if n and seen[q].get(s, 0) < n:
+                eng[q].wait_ge(T.sem[s], n)
+                for s2, n2 in known[d].items():
+                    if seen[q].get(s2, 0) < n2:
+                        seen[q][s2] = n2
+        if q == "G" and o["token"] is None and seen["G"].get("qG", 0) < count["G"]:
+            g.wait_ge(T.sem["qG"], count["G"])
+            seen["G"]["qG"] = count["G"]
+        calls = o["emit"](x, q)
+        if o["token"] is None:
+            for c in calls:
+                count[q] += 1
+                c.then_inc(T.sem["q" + q], 1)
+            tok[i] = ("q" + q, count[q])
+            final["q" + q] = count[q]
+        elif o["token"] == "sent":
+            tok[i] = ("sent", 0)
+        else:
+            calls[0].then_inc(T.sem["d_" + o["token"]], 16)
+            tok[i] = ("d_" + o["token"], 16)
+            final["d_" + o["token"]] = 16
+        known[i] = dict(seen[q])
+        known[i][tok[i][0]] = max(known[i].get(tok[i][0], 0), tok[i][1])
+    final["sent"] = x["sent"][0]
+    for s in sorted(final):
+        if final[s] and seen["G"].get(s, 0) < final[s]:
+            g.wait_ge(T.sem[s], final[s])

@@ -1,48 +1,62 @@
+import math
 from concourse.bass import DstId, RemoteDMATransfer
 from concourse.mybir import AluOpType, ActivationFunctionType
 
 P, S, W, H, TH, DAYS = 2048, 256, 2816, 4096, 11008, 3
 N, U = 512, 4
-GROUPS = [(0, 2), (2, 3), (3, 4)]
-BATCHES = [(0, 4)]
-PAIRED = {(3, 0), (3, 1), (3, 2), (3, 3)}
-TWO = ["xx", "uu"]
+CFG = {
+    "groups": [[(0, 2), (2, 3), (3, 4)]] * 3,
+    "news": [[(0, 2), (2, 3), (3, 4)]] * 3,
+    "batches": [[(0, 4)], [(0, 4)], [(0, 4)]],
+    "slow": [[], [], []],
+    "last_y": 0,
+    "pbank": [0, 1, 2, 0],
+    "hits": 1,
+    "spans": [(0, 1), (1, 2), (2, 3), (3, 4)],
+    "paired": set(),
+    "xbank": [3, 4, 1, 2],
+    "seq": {},
+    "halves": [(0, 2), (2, 4)],
+    "sus_first": 4096,
+    "away_after": 1,
+    "early": 7,
+    "tries": 80000,
+}
 
 SCRATCH = {
     "win1": ("sbuf", [128, W], "bfloat16"), "win2": ("sbuf", [128, W], "bfloat16"), "win3": ("sbuf", [128, W], "bfloat16"),
     "tab": ("sbuf", [128, H], "bfloat16"),
     "shown_i": ("sbuf", [128, 48], "int32"), "shown_u": ("sbuf", [128, 48], "uint16"),
     "c1": ("sbuf", [128, 128], "int32"), "c2": ("sbuf", [128, 128], "int32"), "c3": ("sbuf", [128, 128], "int32"),
-    "c4": ("sbuf", [128, 128], "float32"),
+    "c4": ("sbuf", [128, 128], "int32"), "ho": ("sbuf", [128, 128], "float32"),
     "hu1": ("sbuf", [128, 128], "uint16"), "hu2": ("sbuf", [128, 128], "uint16"), "hu3": ("sbuf", [128, 128], "uint16"),
     "home_i": ("sbuf", [128, 512], "int32"), "away_i": ("sbuf", [128, 512], "int32"), "dif": ("sbuf", [128, 512], "float32"),
     "cu1": ("sbuf", [128, 512], "uint16"), "cu2": ("sbuf", [128, 512], "uint16"), "cu3": ("sbuf", [128, 512], "uint16"),
-    "lowc": ("sbuf", [128, 128], "int32"), "lowx": ("sbuf", [128, 128], "float32"), "ac": ("sbuf", [128, 128], "float32"),
-    "t1": ("sbuf", [128, 128], "float32"), "t2": ("sbuf", [128, 128], "float32"),
-    "hd": ("sbuf", [128, 512], "float32"), "mg": ("sbuf", [128, 512], "float32"),
+    "t1": ("sbuf", [128, 128], "float32"), "t2": ("sbuf", [128, 128], "int32"), "mg": ("sbuf", [128, 512], "float16"),
+    "mid": ("sbuf", [128, 512], "float16"), "ee": ("sbuf", [128, P], "bfloat16"),
     "gc": ("sbuf", [128, 4 * P], "bfloat16"), "gs": ("sbuf", [128, P], "bfloat16"),
     "g0": ("sbuf", [128, P], "float32"), "g2": ("sbuf", [128, P], "float16"),
     "st0": ("sbuf", [128, P], "bfloat16"), "st1": ("sbuf", [128, P], "bfloat16"),
     "sc": ("sbuf", [128, P], "float32"), "fs": ("sbuf", [128, P], "float32"),
     "zi": ("sbuf", [128, 32 * U], "int32"), "zz": ("sbuf", [128, 32 * U], "int32"),
-    "feat": ("sbuf", [128, 96 * U], "bfloat16"), "tts": ("sbuf", [128, 128 * U], "bfloat16"),
+    "feat": ("sbuf", [128, 128 * U], "bfloat16"), "tts": ("sbuf", [128, 128 * U], "bfloat16"),
     "h1": ("sbuf", [128, P], "bfloat16"), "h2": ("sbuf", [128, P], "bfloat16"), "h3": ("sbuf", [128, P], "bfloat16"),
     "hr": ("sbuf", [128, P], "bfloat16"),
     "snd1": ("sbuf", [128, 3 * S], "bfloat16"), "snd2": ("sbuf", [128, 3 * S], "bfloat16"), "snd3": ("sbuf", [128, 3 * S], "bfloat16"),
     "yo": ("sbuf", [128, P], "float32"),
-    "ones": ("sbuf", [128, 128], "bfloat16"), "neg32": ("sbuf", [128, 128], "bfloat16"),
-    "ri": ("sbuf", [128, 128], "bfloat16"), "rih": ("sbuf", [128, 128], "float16"),
-    "ris": ("sbuf", [128, 128], "bfloat16"), "idn": ("sbuf", [128, 128], "bfloat16"),
-    "ev": ("sbuf", [128, 512], "bfloat16"), "em": ("sbuf", [128, 512], "bfloat16"),
-    "mz": ("sbuf", [128, 128], "bfloat16"), "lm": ("sbuf", [128, 512], "bfloat16"),
-    "s1f": ("sbuf", [128, 16], "float32"), "s1q": ("sbuf", [128, 16], "float32"),
-    "d0": ("sbuf", [128, 1024], "float32"),
-    "pp": ("psum", [128, 1024], "float32"), "xx": ("psum", [128, 1024], "float32"), "uu": ("psum", [128, 1024], "float32"),
-    "tl": ("psum", [128, 512], "float32"), "hp": ("psum", [128, 512], "float32"),
+    "ones": ("sbuf", [128, 128], "bfloat16"), "idn": ("sbuf", [128, 128], "bfloat16"), "idh": ("sbuf", [128, 128], "float16"),
+    "d0": ("sbuf", [128, 2048], "bfloat16"),
+    "pi": ("sbuf", [128, 1], "int32"), "fi": ("sbuf", [128, 1], "int32"), "ff": ("sbuf", [128, 1], "float32"),
+    "r4": ("sbuf", [128, 4], "float32"), "hot": ("sbuf", [128, 4], "float32"), "col": ("sbuf", [128, 8], "float32"),
+    "wv": ("sbuf", [128, 128], "float32"), "wa": ("sbuf", [128, 128], "float32"), "wb": ("sbuf", [128, 128], "float32"),
+    "cf": ("sbuf", [128, 128], "bfloat16"), "em": ("sbuf", [128, 512], "bfloat16"),
+    "mz": ("sbuf", [128, 128], "bfloat16"), "sel": ("sbuf", [128, 512], "bfloat16"), "lm": ("sbuf", [128, 3 * 512], "bfloat16"),
+    "xx": ("psum", [128, 2560], "float32"), "bt": ("psum", [128, 2048], "bfloat16"),
+    "tl": ("psum", [128, 512], "float32"),
 }
-BANKS = [n for n in SCRATCH if SCRATCH[n][0] == "psum"]
-DMAS = ["x", "shown", "hist", "sus", "home", "away", "h"] + ["y%d" % u for u in range(U)]
-SEMAPHORES = ["q" + q for q in "VSPG"] + ["d_" + n for n in DMAS] + ["arr1", "arr2", "arr3", "sent"]
+BANKS = {n: (1024 if SCRATCH[n][2] == "bfloat16" else 512) for n in SCRATCH if SCRATCH[n][0] == "psum"}
+DMAS = ["x", "shown", "hist", "sus0", "sus1", "home", "away"] + ["y%d" % u for u in range(U + 1)] + ["h%d" % u for u in range(U)]
+SEMAPHORES = ["q" + q for q in "VSPG"] + ["d_" + n for n in DMAS] + ["arr1", "arr2", "arr3", "sent", "issued"]
 
 
 def routes(T, topo, core):
@@ -60,10 +74,10 @@ def build_graph():
     ops, seen = [], {}
     A, F = AluOpType, ActivationFunctionType
 
-    def op(cost, emit, rd=(), wr=(), lat=None, token=None, group=None, deps=()):
+    def op(name, cost, emit, rd=(), wr=(), lat=None, token=None, group=None, deps=()):
         i, dep = len(ops), set(deps)
         acc = [(r, False) for r in rd] + [(r, True) for r in wr]
-        acc = [((b, lo // 512 * 512, -(-hi // 512) * 512), True) if b in BANKS else ((b, lo, hi), w) for (b, lo, hi), w in acc]
+        acc = [((b, lo // BANKS[b] * BANKS[b], -(-hi // BANKS[b]) * BANKS[b]), True) if b in BANKS else ((b, lo, hi), w) for (b, lo, hi), w in acc]
         for (b, lo, hi), w in acc:
             for l2, h2, j, w2, g2 in seen.get(b, ()):
                 if l2 < hi and lo < h2 and (w or w2) and j != i and (group is None or g2 != group):
@@ -73,63 +87,89 @@ def build_graph():
             if w and group is None:
                 old[:] = [t for t in old if not (lo <= t[0] and t[1] <= hi)]
             old.append((lo, hi, i, w, group))
-        ops.append({"cost": cost, "emit": emit, "deps": sorted(dep), "lat": lat, "token": token})
+        ops.append({"name": name, "cost": cost, "emit": emit, "deps": sorted(dep), "needs": sorted(dep), "lat": lat, "token": token})
         return i
 
     def v(n, c=1.0): return {"V": (1, max(64, n * c), 0, 0)}
-    def vs(n, c=1.0): return {"V": (1, n * c, 0, 0), "S": (1, n, 0, 0)}
+    def vs(n, c=1.0): return {"V": (1, max(64, n * c), 0, 0), "S": (1, max(64, n), 0, 0)}
     def gat(n): return {"V": (1, 0, n, 0), "S": (1, 0, n, 0)}
     def pe(k, n): return {"P": (k, 0, 0, k * max(64, n))}
     def gp(n): return {"G": (2, 2 * n, 0, 0)}
 
-    def load(name, dst, lo, hi, q, kb):
-        op({q: (1, 0, 0, 0)}, lambda x, q: [x["eng"][q].dma_start(x["T"][dst][:, lo:hi], x["T"][name][:])], wr=[(dst, lo, hi)], lat=("dma", kb), token=name)
+    def load(name, src, dst, lo, hi, q, kb, deps=()):
+        op("load " + name, {q: (1, 0, 0, 0)}, lambda x, q: [x["eng"][q].dma_start(x["T"][dst][:, lo:hi], x["T"][src][:, lo:hi])], wr=[(dst, lo, hi)],
+           lat=("dma", kb, 128), token=name, deps=deps)
 
-    load("shown", "shown_i", 0, 48, "S", 24)
-    load("x", "win1", 0, P, "Y", 512)
-    load("hist", "c1", 0, 128, "S", 64)
-    load("sus", "tab", 0, H, "Y", 1600)
-    load("home", "home_i", 0, 512, "S", 800)
-    load("away", "away_i", 0, 512, "Y", 2100)
+    cut = CFG["sus_first"]
+    load("shown", "shown", "shown_i", 0, 48, "S", 24)
+    load("x", "x", "win1", 0, P, "Y", 512)
+    load("hist", "hist", "c1", 0, 128, "S", 64)
+    load("home", "home", "home_i", 0, 512, "Y", 256)
+    if cut:
+        load("sus0", "sus", "tab", 0, cut, "Y", cut // 4)
 
-    def fill(buf, rows, lo, hi, val, key=None, step=1):
-        op(v((hi - lo) // step), lambda x, q: [x["v"].memset(x["T"][buf][rows[0]:rows[1], lo:hi:step], val)], wr=[(key or buf, 0 if step > 1 else lo, hi)])
+    def fill(buf, lo, hi, val, key=None, step=1):
+        op("fill " + buf, v((hi - lo) // step, 0.5), lambda x, q: [x["v"].memset(x["T"][buf][:, lo:hi:step], val)], wr=[(key or buf, 0 if step > 1 else lo, hi)])
 
-    def select(buf, src, rows, lo, hi, slo, shi, pattern, base, cm, rkey, wkey):
-        op(gp(hi - lo), lambda x, q: [x["g"].affine_select(x["T"][buf][rows[0]:rows[1], lo:hi], x["T"][src][rows[0]:rows[1], slo:shi], pattern, A.is_equal, 0.0, base, cm)],
-           rd=[(rkey, slo, shi)], wr=[(wkey, lo, hi)])
+    def select(buf, lo, hi, src, slo, pattern, how, base, cm):
+        op("select " + buf, gp(hi - lo), lambda x, q: [x["g"].affine_select(x["T"][buf][:, lo:hi], x["T"][src][:, slo:slo + hi - lo], pattern, how, 0.0, base, cm)],
+           rd=[(src, slo, slo + hi - lo)], wr=[(buf, lo, hi)])
 
-    def iota(buf, rows, n, pattern, base, key):
-        op(gp(n), lambda x, q: [x["g"].iota(x["T"][buf][rows[0]:rows[1], 0:n], pattern, base, 0, allow_small_or_imprecise_dtypes=True)], wr=[(key, 0, n)])
+    def iota(buf, n, pattern, base, cm):
+        kw = {} if SCRATCH[buf][2] == "int32" else {"allow_small_or_imprecise_dtypes": True}
+        op("iota " + buf, gp(n), lambda x, q: [x["g"].iota(x["T"][buf][:, 0:n], pattern, base, cm, **kw)], wr=[(buf, 0, n)])
 
-    full = (0, 128)
-    fill("ones", full, 0, 128, 1.0)
-    fill("neg32", full, 0, 128, -32.0)
-    select("idn", "ones", full, 0, 128, 0, 128, [[-1, 128]], 0, 1, "ones", "idn")
-    select("ri", "ones", full, 0, 128, 0, 128, [[-16, 8], [1, 16]], -15, 1, "ones", "ri")
-    select("ris", "neg32", full, 0, 128, 0, 128, [[-16, 8], [1, 16]], -15, 1, "neg32", "ris")
-    op(v(128), lambda x, q: [x["v"].tensor_copy(x["T"].rih[:], x["T"].ri[:])], rd=[("ri", 0, 128)], wr=[("rih", 0, 128)])
-    fill("d0", full, 0, 1024, 1.0)
-    fill("d0", full, 0, 1024, 16777216.0, step=16)
-    fill("feat", full, 64, 96 * U, 1.0, step=96, key="one")
-    iota("s1f", (64, 96), 16, [[1, 16]], 1, "s1f")
-    iota("ev", (0, 32), 512, [[0, 32], [128, 16]], 128, "ev0")
-    fill("ev", (32, 64), 0, 512, -64.0, key="ev1")
-    op(v(16), lambda x, q: [x["v"].tensor_tensor(x["T"].s1q[64:96, :], x["T"].s1f[64:96, :], x["T"].s1f[64:96, :], A.mult)], rd=[("s1f", 0, 16)], wr=[("s1q", 0, 16)])
-    op(v(16), lambda x, q: [x["v"].tensor_scalar(x["T"].em[64:96, 0:16], x["T"].s1q[64:96, :], -64.0, 64.0, A.mult, A.add)], rd=[("s1q", 0, 16)], wr=[("em2", 0, 16)])
-    for w in (16, 32, 64, 128, 256):
-        op(v(w), lambda x, q, w=w: [x["v"].tensor_copy(x["T"].em[64:96, w:2 * w], x["T"].em[64:96, 0:w])], rd=[("em2", 0, w)], wr=[("em2", w, 2 * w)])
-    for f in range(2):
-        select("em", "ev", (32 * f, 32 * f + 32), 0, 512, 0, 512, [[-8, 4], [-1, 8], [0, 16]], 0, 1, "ev%d" % f, "em%d" % f)
-    EM = [("em0", 0, 512), ("em1", 0, 512), ("em2", 0, 512)]
-    select("mz", "ones", (0, 32), 0, 128, 0, 128, [[-1, 8], [0, 4], [-8, 4]], 0, 1, "ones", "mz")
-    for h in range(4):
-        select("lm", "mz", (0, 32), 128 * h, 128 * h + 128, 0, 128, [[0, 8], [1, 4], [0, 4]], -h, 0, "mz", "lm")
+    def ts(name, out, lo, hi, src, slo, s1, s2, o0, o1=None, c=1.0):
+        cols = [s for s in (s1, s2) if isinstance(s, tuple)]
+
+        def emit(x, q):
+            T = x["T"]
+            a, b = [T[s[0]][:, s[1]:s[1] + 1] if isinstance(s, tuple) else s for s in (s1, s2)]
+            return [x["v"].tensor_scalar(T[out][:, lo:hi], T[src][:, slo:slo + hi - lo], a, b, *([o0] if o1 is None else [o0, o1]))]
+        return op(name, v(hi - lo, c), emit, rd=[(src, slo, slo + hi - lo)] + [(b, j, j + 1) for b, j in cols], wr=[(out, lo, hi)])
+
+    def tt(name, out, lo, hi, a, alo, b, blo, o):
+        c = 1.0 if a in BANKS or b in BANKS else 2.0
+        return op(name, v(hi - lo, c), lambda x, q: [x["v"].tensor_tensor(x["T"][out][:, lo:hi], x["T"][a][:, alo:alo + hi - lo], x["T"][b][:, blo:blo + hi - lo], o)],
+                  rd=[(a, alo, alo + hi - lo), (b, blo, blo + hi - lo)], wr=[(out, lo, hi)])
 
     def copy(dst, src, lo, hi):
-        op(v(hi - lo), lambda x, q: [x["v"].tensor_copy(x["T"][dst][:, lo:hi], x["T"][src][:, lo:hi])], rd=[(src, lo, hi)], wr=[(dst, lo, hi)])
+        op("copy %s %d" % (dst, lo // 32), v(hi - lo), lambda x, q: [x["v"].tensor_copy(x["T"][dst][:, lo:hi], x["T"][src][:, lo:hi])], rd=[(src, lo, hi)], wr=[(dst, lo, hi)])
 
-    def gather(dst, lo, hi, win, whi, lst, llo, bias, lkey=None):
+    fill("ones", 0, 128, 1.0)
+    select("idn", 0, 128, "ones", 0, [[-1, 128]], A.is_equal, 0, 1)
+    if CFG["paired"]:
+        copy("idh", "idn", 0, 128)
+    wide = N * max(b - a for day in CFG["groups"] for a, b in day)
+    fill("d0", 0, wide, 1.0 / 32)
+    fill("d0", 0, wide, -1048576.0, step=16)
+    fill("feat", 3, 128 * U, 1.0, step=4, key="one")
+    iota("pi", 1, [[1, 1]], 0, 1)
+    iota("r4", 4, [[1, 4]], 0, 0)
+    iota("wv", 128, [[0, 8], [-1, 16]], 15, 0)
+    ts("const", "fi", 0, 1, "pi", 0, 3, None, A.bitwise_and)
+    copy("ff", "fi", 0, 1)
+    ts("const", "hot", 0, 4, "r4", 0, ("ff", 0), None, A.is_equal)
+    ts("const", "col", 0, 1, "hot", 3, -64.0, None, A.mult)
+    ts("const", "col", 1, 2, "hot", 0, 128.0, None, A.mult)
+    ts("const", "col", 2, 3, "hot", 3, ("hot", 1), 64.0, A.subtract, A.mult)
+    ts("const", "col", 3, 4, "hot", 2, 15.0, ("hot", 3), A.mult, A.add)
+    ts("const", "col", 4, 5, "hot", 3, 16.0, ("hot", 0), A.mult, A.subtract)
+    ts("const", "col", 5, 6, "col", 4, ("hot", 2), None, A.subtract)
+    ts("const", "wa", 0, 128, "wv", 0, ("col", 0), ("col", 1), A.mult, A.add)
+    tt("const", "wb", 0, 128, "wa", 0, "wv", 0, A.mult)
+    ts("const", "cf", 0, 128, "wb", 0, ("col", 2), None, A.add)
+    for r in range(4):
+        select("em", 128 * r, 128 * r + 128, "cf", 0, [[-4, 8], [0, 16]], A.is_ge, -32 * r, 1)
+    select("em", 0, 512, "em", 0, [[32, 4], [4, 8], [0, 16]], A.is_ge, 3, -1)
+    select("mz", 0, 128, "ones", 0, [[-4, 8], [0, 4], [-32, 4]], A.is_ge, 0, 1)
+    select("mz", 0, 128, "mz", 0, [[4, 8], [0, 4], [32, 4]], A.is_ge, 3, -1)
+    for h in range(4):
+        select("sel", 128 * h, 128 * h + 128, "mz", 0, [[0, 8], [1, 4], [0, 4]], A.is_equal, -h, 0)
+    for j, c in enumerate((("col", 3), ("col", 5), ("hot", 2))):
+        ts("const lm", "lm", 512 * j, 512 * j + 512, "sel", 0, c, None, A.mult, c=0.5)
+
+    def gather(name, dst, lo, hi, win, whi, lst, llo, bias, lkey=None):
         k = (hi - lo) // 16
 
         def emit(x, q):
@@ -140,15 +180,22 @@ def build_graph():
                 return [x["s"].activation(o, w, F.Identity, bias=bias)] if bias else [x["s"].activation(o, w, F.Copy)]
             return [x["v"].tensor_scalar(o, w, bias, None, A.add)] if bias else [x["v"].tensor_copy(o, w)]
         lr = (lst, llo, llo + k) if lkey is None else (lst,) + lkey
-        return op(gat(hi - lo), emit, rd=[(win, 0, whi), lr], wr=[(dst, lo, hi)])
+        return op(name, gat(hi - lo), emit, rd=[(win, 0, whi), lr], wr=[(dst, lo, hi)])
+
+    def move(name, dst, lo, hi, src, slo, c):
+        def emit(x, q):
+            o, w = x["T"][dst][:, lo:hi], x["T"][src][:, slo:slo + hi - lo]
+            return [x["s"].activation(o, w, F.Copy)] if q == "S" else [x["v"].tensor_copy(o, w)]
+        op(name, vs(hi - lo, c), emit, rd=[(src, slo, slo + hi - lo)], wr=[(dst, lo, hi)])
 
     def send(d):
         win, snd, arr = "win%d" % d, "snd%d" % d, "arr%d" % d
+        got = []
         for i in range(3):
             def llo(x, i=i):
                 to = [t for call in x["routes"] for t in call][i][0]
                 return 16 * part(x["rank"], x["T"].rank_of(to))
-            gather(snd, S * i, S * i + S, win, P, "shown_u", llo, 0.0, lkey=(0, 48))
+            got.append(gather("slot %d %d" % (d, i), snd, S * i, S * i + S, win, P, "shown_u", llo, 0.0, lkey=(0, 48)))
         calls, pos = [], 0
         for n, size in enumerate((2, 1)):
             def emit(x, q, n=n, pos=pos):
@@ -165,180 +212,231 @@ def build_graph():
                     x["g"].remote_dma_fused([RemoteDMATransfer(dst_ids=[DstId(rid=r, pnc=p)], dma_engine_mask=m, remote_sem=T.sem[arr], srcs=[a], dsts=[o])
                                              for r, p, o, a, m in trs], local_sem=T.sem["sent"])
                 return []
-            calls.append(op({"G": (12, 0, 0, 0)}, emit, rd=[(snd, S * pos, S * (pos + size))], lat=("remote", 64 * size), token="sent"))
+            calls.append(op("send %d %d" % (d, n), {"G": (0, 0, 0, 0, 1)}, emit, rd=[(snd, S * pos, S * (pos + size))],
+                            lat=("remote", 64 * size, 128 * size), token="sent"))
             pos += size
-        return op({"-": (0, 0, 0, 0)}, None, wr=[(win, P, W)], token=arr, deps=calls)
+        issued = None
+        if d == 1 and cut < H:
+            issued = op("issued", {"G": (1, 0, 0, 0)}, lambda x, q: [x["g"].sem_inc(x["T"].sem["issued"], 1)], token="issued")
+        return issued, op("landed %d" % d, {"-": (0, 0, 0, 0)}, None, wr=[(win, P, W)], token=arr, deps=calls)
 
-    def tables(d, u):
-        i0, e, st, b, uu = N * u, N * u + N, "st%d" % (d % 2), N * (u % 2), TWO[u // 2]
-        gather("gs", i0, e, "tab", H, "hu%d" % d, i0 // 16, 0.0)
-        op(pe(4, 128), lambda x, q: [x["t"].matmul(x["T"][uu][:, b + 128 * k:b + 128 * k + 128], x["T"].gs[:, i0 + k:e:4], x["T"].ris[:], True, True) for k in range(4)],
-           rd=[("gs", i0, e), ("ris", 0, 128)], wr=[(uu, b, b + N)])
+    def tables(d, u0, u1):
+        st = "st%d" % (d % 2)
+        for u in range(u0, u1):
+            i0, e = N * u, N * u + N
+            gather("sus %d %d" % (d, u), "gs", i0, e, "tab", H, "hu%d" % d, i0 // 16, 0.0)
+            op("turn sus %d %d" % (d, u), pe(4, 128),
+               lambda x, q, i0=i0, e=e: [x["t"].transpose(x["T"].bt[:, i0 + 128 * k:i0 + 128 * k + 128], x["T"].gs[:, i0 + k:e:4], x["T"].idn[:]) for k in range(4)],
+               rd=[("gs", i0, e), ("idn", 0, 128)], wr=[("bt", i0, e)])
+            if u % 2 or u == u1 - 1:
+                lo = max(N * u0, N * (u - u % 2))
+                move("down sus %d %d" % (d, u), st, lo, e, "bt", lo, 0.5)
 
-        def out(x, q):
-            o, w = x["T"][st][:, i0:e], x["T"][uu][:, b:b + N]
-            return [x["s"].activation(o, w, F.Copy)] if q == "S" else [x["v"].tensor_copy(o, w)]
-        op(vs(N), out, rd=[(uu, b, b + N)], wr=[(st, i0, e)])
-
-    def halves(d, u):
-        i0, e, dst, win = N * u, N * u + N, "h%d" % d, "win%d" % d
+    def halves(d, u0, u1):
+        i0, e, dst, win = N * u0, N * u1, "h%d" % d, "win%d" % d
         to = dst if d < DAYS else "hr"
         add = -255.375 if d == 1 else -127.875
 
         def emit(x, q):
             o, w = x["T"][to][:, i0:e], x["T"][win][:, i0:e]
             return [x["s"].activation(o, w, F.Identity, bias=add, scale=0.5)] if q == "S" else [x["v"].tensor_scalar(o, w, 0.5, add, A.mult, A.add)]
-        op(vs(N, 0.5), emit, rd=[(win, i0, e)], wr=[(to, i0, e)])
+        op("half %d %d" % (d, u0), vs(e - i0, 0.5), emit, rd=[(win, i0, e)], wr=[(to, i0, e)])
         if d == DAYS:
             def back(x, q):
                 o, w = x["T"][dst][:, i0:e], x["T"].hr[:, i0:e]
                 return [x["s"].activation(o, w, F.Identity, bias=255.0)] if q == "S" else [x["v"].tensor_scalar(o, w, 255.0, None, A.add)]
-            op(vs(N, 0.5), back, rd=[("hr", i0, e)], wr=[(dst, i0, e)])
+            op("back %d" % u0, vs(e - i0, 0.5), back, rd=[("hr", i0, e)], wr=[(dst, i0, e)])
 
     def base(d, u):
-        i0, e, hh, uu, b = N * u, N * u + N, "h%d" % d, TWO[u // 2], N * (u % 2)
-        op(pe(1, N), lambda x, q: [x["t"].matmul(x["T"][uu][:, b:b + N], x["T"].idn[:], x["T"][hh][:, i0:e], True, False)],
-           rd=[(hh, i0, e), ("idn", 0, 128)], wr=[(uu, b, b + N)])
+        i0, e, hh, b = N * u, N * u + N, "h%d" % d, N * CFG["xbank"][u]
+        op("base %d %d" % (d, u), pe(1, N), lambda x, q: [x["t"].matmul(x["T"].xx[:, b:b + N], x["T"].idn[:], x["T"][hh][:, i0:e], True, False)],
+           rd=[(hh, i0, e), ("idn", 0, 128)], wr=[("xx", b, b + N)])
 
-    def low(d):
-        c = "c%d" % d
-        op(v(128), lambda x, q: [x["v"].tensor_scalar(x["T"].lowc[:], x["T"][c][:], 255, None, A.bitwise_and)], rd=[(c, 0, 128)], wr=[("lowc", 0, 128)])
-        op(v(128), lambda x, q: [x["v"].tensor_scalar(x["T"].lowx[:], x["T"].lowc[:], 16.0, -1.0, A.mult, A.add)], rd=[("lowc", 0, 128)], wr=[("lowx", 0, 128)])
-        op(v(128, 2), lambda x, q: [x["v"].tensor_tensor(x["T"].ac[:], x["T"].lowx[:], x["T"][c][:], A.subtract)], rd=[("lowx", 0, 128), (c, 0, 128)], wr=[("ac", 0, 128)])
-
-    def pressure(d, u):
-        i0, e, b, win, cu = N * u, N * u + N, N * (u % 2), "win%d" % d, "cu%d" % d
+    def contacts(d, u0, u1):
+        i0, e, win, cu = N * u0, N * u1, "win%d" % d, "cu%d" % d
         bias = 0.0 if d == 1 else 255.0
-        pieces = []
-        mine = [c for c in range(4) if (c, u) in PAIRED]
+        mine = [c for c in range(4) if (c, u0) in CFG["paired"]]
         for c in range(4):
-            a = 128 * c + i0 // 16
+            a, name = 128 * c + i0 // 16, "con %d %d %d" % (d, u0, c)
             if mine and c == 0:
-                gather("g0", i0, e, win, W, cu, a, 2 * bias)
-                pieces.append(("g2", 0, "rih"))
+                gather(name, "g0", i0, e, win, W, cu, a, 2 * bias)
             elif c in mine:
-                op({"V": (1, 0, N, 0)},
-                   lambda x, q, a=a: [x["v"].tensor_tensor(x["T"].g2[:, i0:e], x["T"][win][:, 0:W].indirect(x["T"][cu][:, a:a + N // 16]), x["T"].g0[:, i0:e], A.add)],
-                   rd=[(win, 0, W), (cu, a, a + N // 16), ("g0", i0, e)], wr=[("g2", i0, e)])
+                op(name, {"V": (1, 0, e - i0, 0)},
+                   lambda x, q, a=a: [x["v"].tensor_tensor(x["T"].g2[:, i0:e], x["T"][win][:, 0:W].indirect(x["T"][cu][:, a:a + (e - i0) // 16]), x["T"].g0[:, i0:e], A.add)],
+                   rd=[(win, 0, W), (cu, a, a + (e - i0) // 16), ("g0", i0, e)], wr=[("g2", i0, e)])
             else:
-                gather("gc", P * c + i0, P * c + e, win, W, cu, a, bias)
-                pieces.append(("gc", P * c, "ri"))
-        last = len(pieces) - 1
+                gather(name, "gc", P * c + i0, P * c + e, win, W, cu, a, bias)
+        return [("g2", 0, "idh") if c in mine else ("gc", P * c, "idn") for c in range(4) if not (mine and c == 0)]
+
+    def pressure(d, u, pieces):
+        b, last = N * CFG["pbank"][u], len(pieces) - 1
         for buf, at, idn in pieces:
-            def emit(x, q, buf=buf, at=at + i0, idn=idn):
+            def emit(x, q, buf=buf, at=at + N * u, idn=idn):
                 T, key = x["T"], (d, u)
                 t = x["open"].get(key, 0)
                 x["open"][key] = t + 1
-                return [x["t"].matmul(T.pp[:, b + 128 * k:b + 128 * k + 128], T[buf][:, at + k:at + N:4], T[idn][:], t == 0 and k == 0, t == last and k == 3) for k in range(4)]
-            op(pe(4, 128), emit, rd=[(buf, at + i0, at + e), (idn, 0, 128)], wr=[("pp", b, b + N)], group=(d, u))
+                return [x["t"].matmul(T.xx[:, b + 128 * k:b + 128 * k + 128], T[buf][:, at + k:at + N:4], T[idn][:], t == 0 and k == 0, t == last and k == 3) for k in range(4)]
+            op("add %d %d %d" % (d, u, at // P), pe(4, 128), emit, rd=[(buf, at + N * u, at + N * u + N), (idn, 0, 128)], wr=[("xx", b, b + N)], group=(d, u))
 
     def outcome(d, u0, u1):
-        i0, e, n, m0, m1 = N * u0, N * u1, N * (u1 - u0), 32 * u0, 32 * u1
-        st, hh, k, uu, b = "st%d" % (d % 2), "h%d" % d, u1 - u0, TWO[u0 // 2], N * (u0 % 2)
-        op(v(n), lambda x, q: [x["v"].tensor_tensor(x["T"].sc[:, i0:e], x["T"].pp[:, b:b + n], x["T"][st][:, i0:e], A.mult)], rd=[("pp", b, b + n), (st, i0, e)], wr=[("sc", i0, e)])
-        op(v(n), lambda x, q: [x["v"].tensor_tensor_scan(x["T"].fs[:, i0:e], x["T"].d0[:, 0:n], x["T"].sc[:, i0:e], 0.0, A.add, A.min)], rd=[("sc", i0, e), ("d0", 0, 1024)], wr=[("fs", i0, e)])
-        op(v(32 * k), lambda x, q: [x["v"].tensor_scalar(x["T"].zi[:, m0:m1], x["T"].fs[:, i0 + 15:e:16], 1.0, -32.0 * TH, A.add, A.min)], rd=[("fs", i0, e)], wr=[("zi", m0, m1)])
-        op(v(32 * k), lambda x, q: [x["v"].tensor_scalar(x["T"].zz[:, m0:m1], x["T"].zi[:, m0:m1], 31, None, A.bitwise_and)], rd=[("zi", m0, m1)], wr=[("zz", m0, m1)])
-        for u in range(u0, u1):
-            a, f, j = 32 * u, 96 * u, 128 * (u - u0)
-            op(v(32), lambda x, q, a=a, f=f: [x["v"].tensor_copy(x["T"].feat[:, f:f + 32], x["T"].zz[:, a:a + 32])], rd=[("zz", a, a + 32)], wr=[("feat", f, f + 32)])
-            op(v(32, 2), lambda x, q, a=a, f=f: [x["v"].tensor_tensor(x["T"].feat[:, f + 32:f + 64], x["T"].zz[:, a:a + 32], x["T"].zz[:, a:a + 32], A.mult)],
-               rd=[("zz", a, a + 32)], wr=[("feat", f + 32, f + 64)])
-            op(pe(1, 128), lambda x, q, f=f, j=j: [x["t"].matmul(x["T"].tl[0:65, j:j + 128], x["T"].feat[:, f:f + 65], x["T"].idn[:], True, True)],
-               rd=[("feat", f, f + 65), ("one", 0, 96 * U), ("idn", 0, 128)], wr=[("tl", 0, 512)])
+        i0, e, n, m0, m1, f0, f1 = N * u0, N * u1, N * (u1 - u0), 32 * u0, 32 * u1, 128 * u0, 128 * u1
+        st, k, b, tag = "st%d" % (d % 2), u1 - u0, N * CFG["pbank"][u0], " %d %d" % (d, u0)
+        tt("score" + tag, "sc", i0, e, "xx", b, st, i0, A.mult)
+        op("scan" + tag, v(n), lambda x, q: [x["v"].tensor_tensor_scan(x["T"].fs[:, i0:e], x["T"].d0[:, 0:n], x["T"].sc[:, i0:e], 0.0, A.add, A.max)],
+           rd=[("sc", i0, e), ("d0", 0, n)], wr=[("fs", i0, e)])
+        op("best" + tag, v(32 * k), lambda x, q: [x["v"].tensor_scalar(x["T"].zi[:, m0:m1], x["T"].fs[:, i0 + 15:e:16], 32.0, 32.0 * TH + 16, A.mult, A.max)],
+           rd=[("fs", i0, e)], wr=[("zi", m0, m1)])
+        op("hit" + tag, v(32 * k), lambda x, q: [x["v"].tensor_scalar(x["T"].feat[:, f0 + 2:f1:4], x["T"].fs[:, i0 + 15:e:16], TH + 0.75, None, A.is_gt)],
+           rd=[("fs", i0, e)], wr=[("f2", f0, f1)])
+        ts("w" + tag, "zz", m0, m1, "zi", m0, 31, None, A.bitwise_and)
+        op("w1" + tag, v(32 * k), lambda x, q: [x["v"].tensor_copy(x["T"].feat[:, f0:f1:4], x["T"].zz[:, m0:m1])], rd=[("zz", m0, m1)], wr=[("f0", f0, f1)])
+        op("w2" + tag, v(32 * k, 2), lambda x, q: [x["v"].tensor_tensor(x["T"].feat[:, f0 + 1:f1:4], x["T"].zz[:, m0:m1], x["T"].zz[:, m0:m1], A.mult)],
+           rd=[("zz", m0, m1)], wr=[("f1", f0, f1)])
+        op("turn w" + tag, pe(k, 128),
+           lambda x, q: [x["t"].transpose(x["T"].bt[:, 1024 + 128 * j:1024 + 128 * j + 128], x["T"].feat[:, f0 + 128 * j:f0 + 128 * j + 128], x["T"].idn[:]) for j in range(k)],
+           rd=[("f0", f0, f1), ("f1", f0, f1), ("f2", f0, f1), ("one", 0, 128 * U), ("idn", 0, 128)], wr=[("bt", 1024, 1024 + 128 * k)])
+        move("down w" + tag, "tts", f0, f1, "bt", 1024, 0.5)
 
-        def down(x, q):
-            o, w = x["T"].tts[0:65, 128 * u0:128 * u1], x["T"].tl[0:65, 0:128 * k]
-            return [x["s"].activation(o, w, F.Copy)] if q == "S" else [x["v"].tensor_copy(o, w)]
-        op(vs(128 * k), down, rd=[("tl", 0, 512)], wr=[("tts", 128 * u0, 128 * u1)])
+    def renew(d, u0, u1):
+        i0, e, tag, b, hh = N * u0, N * u1, " %d %d" % (d, u0), N * CFG["xbank"][u0], "h%d" % d
+        slow = u0 in CFG["slow"][d - 1]
         for u in range(u0, u1):
-            j, t = N * (u % 2), 128 * u
-            op(pe(4, 128), lambda x, q, j=j, t=t: [x["t"].matmul(x["T"][uu][:, j + r:j + N:4], x["T"].em[0:65, 128 * r:128 * r + 128], x["T"].tts[0:65, t:t + 128], False, r == 3)
-                                                   for r in range(4)], rd=[("tts", t, t + 128)] + EM, wr=[(uu, j, j + N)])
+            j, t = N * CFG["xbank"][u], 128 * u
+            if not slow:
+                base(d, u)
+            op("spread %d %d" % (d, u), pe(4, 128),
+               lambda x, q, j=j, t=t: [x["t"].matmul(x["T"].xx[:, j + r:j + N:4], x["T"].em[:, 128 * r:128 * r + 128], x["T"].tts[:, t:t + 128], slow and r == 0, r == 3)
+                                       for r in range(4)],
+               rd=[("tts", t, t + 128), ("em", 0, 512)], wr=[("xx", j, j + N)])
         to = "win%d" % (d + 1) if d < DAYS else "yo"
-        op(v(n), lambda x, q: [x["v"].tensor_tensor(x["T"][to][:, i0:e], x["T"][uu][:, b:b + n], x["T"][hh][:, i0:e], A.max)], rd=[(uu, b, b + n), (hh, i0, e)], wr=[(to, i0, e)])
-        if d == DAYS:
-            op({"Y": (1, 0, 0, 0)}, lambda x, q: [x["y"].dma_start(x["T"].y[:, i0:e], x["T"].yo[:, i0:e])], rd=[("yo", i0, e)], lat=("dma", 256 * k), token="y%d" % u0)
+        if slow:
+            def cut(x, q):
+                o, w = x["T"].ee[:, i0:e], x["T"].xx[:, b:b + e - i0]
+                return [x["s"].activation(o, w, F.Relu)] if q == "S" else [x["v"].tensor_scalar(o, w, 0.0, None, A.max)]
+            op("caught" + tag, vs(e - i0), cut, rd=[("xx", b, b + e - i0)], wr=[("ee", i0, e)])
+            for u in range(u0, u1):
+                j, a = N * CFG["xbank"][u], N * u
+                op("sum %d %d" % (d, u), pe(2, N),
+                   lambda x, q, j=j, a=a: [x["t"].matmul(x["T"].xx[:, j:j + N], x["T"].idn[:], x["T"][src][:, a:a + N], src == hh, src != hh) for src in (hh, "ee")],
+                   rd=[(hh, a, a + N), ("ee", a, a + N), ("idn", 0, 128)], wr=[("xx", j, j + N)])
+            move("new" + tag, to, i0, e, "xx", b, 1.0)
+        cuts = [i0, e] if d < DAYS or u1 < U else [i0, e - CFG["last_y"], e]
+        for n, (lo, hi) in enumerate(zip(cuts, cuts[1:])):
+            if lo == hi:
+                continue
+            if not slow:
+                tt("new" + tag, to, lo, hi, "xx", b + lo - i0, hh, lo, A.max)
+            if d == DAYS:
+                op("store y %d" % u0, {"YS"[n]: (1, 0, 0, 0)}, lambda x, q, lo=lo, hi=hi: [x["eng"][q].dma_start(x["T"].y[:, lo:hi], x["T"].yo[:, lo:hi])], rd=[("yo", lo, hi)],
+                   lat=("dma", (hi - lo) // 2, 128), token="y%d" % (u0 + n))
+
+    def listed(d, j, u0, u1):
+        lo, hi = 128 * j + 32 * u0, 128 * j + 32 * u1
+        op("list %d %d %d" % (d, j, u0), pe(4, hi - lo),
+           lambda x, q: [x["t"].matmul(x["T"].tl[:, lo:hi], x["T"].lm[:, 512 * j + 128 * h:512 * j + 128 * h + 128], x["T"].tts[:, 128 * u0 + h:128 * u1:4], h == 0, h == 3)
+                         for h in range(4)], rd=[("tts", 128 * u0, 128 * u1), ("lm", 512 * j, 512 * j + 512)], wr=[("tl", lo, hi)])
 
     def histories(d, u0, u1):
-        lo, hi, k = 32 * u0, 32 * u1, 32 * (u1 - u0)
-        z0, h0 = 256, 384
-        op(pe(4, k), lambda x, q: [x["t"].matmul(x["T"].tl[:, z0 + lo:z0 + hi], x["T"].lm[0:32, 128 * h:128 * h + 128], x["T"].tts[0:32, 128 * u0 + h:128 * u1:4], h == 0, h == 3)
-                                   for h in range(4)], rd=[("tts", 128 * u0, 128 * u1), ("lm", 0, 512)], wr=[("tl", 0, 512)])
-        c, cn, hu = "c%d" % d, "c%d" % (d + 1), "hu%d" % (d + 1)
-        op(v(k), lambda x, q: [x["v"].tensor_scalar(x["T"].tl[:, h0 + lo:h0 + hi], x["T"].tl[:, z0 + lo:z0 + hi], 1.0, None, A.min)], wr=[("tl", 0, 512)])
-        op(v(k), lambda x, q: [x["v"].tensor_tensor(x["T"].t1[:, lo:hi], x["T"].tl[:, h0 + lo:h0 + hi], x["T"].ac[:, lo:hi], A.mult)], rd=[("tl", 0, 512), ("ac", lo, hi)], wr=[("t1", lo, hi)])
-        op(v(k), lambda x, q: [x["v"].tensor_tensor(x["T"].t2[:, lo:hi], x["T"].tl[:, z0 + lo:z0 + hi], x["T"].t1[:, lo:hi], A.add)], rd=[("tl", 0, 512), ("t1", lo, hi)], wr=[("t2", lo, hi)])
-        op(v(k, 2), lambda x, q: [x["v"].tensor_tensor(x["T"][cn][:, lo:hi], x["T"].t2[:, lo:hi], x["T"][c][:, lo:hi], A.add)], rd=[("t2", lo, hi), (c, lo, hi)], wr=[(cn, lo, hi)])
-        if d < DAYS:
-            copy(hu, cn, lo, hi)
+        lo, hi, tag = 32 * u0, 32 * u1, " %d %d" % (d, u0)
+        listed(d, 0, u0, u1)
+        listed(d, 1, u0, u1)
+        tt("hist a" + tag, "t1", lo, hi, "tl", lo, "c%d" % d, lo, A.mult)
+        tt("hist b" + tag, "t2", lo, hi, "tl", 128 + lo, "t1", lo, A.add)
+        ts("hist c" + tag, "c%d" % (d + 1), lo, hi, "t2", lo, H - 1, None, A.bitwise_and)
+        copy("hu%d" % (d + 1) if d < DAYS else "ho", "c%d" % (d + 1), lo, hi)
+        if d == DAYS:
+            op("store h %d" % u0, {"Y": (1, 0, 0, 0), "S": (1, 0, 0, 0)}, lambda x, q: [x["eng"][q].dma_start(x["T"].h[:, lo:hi], x["T"].ho[:, lo:hi])], rd=[("ho", lo, hi)],
+               lat=("dma", (hi - lo) // 2, 128), token="h%d" % u0)
 
-    def contacts(d):
+    def lists(d):
+        listed(d - 1, 2, 0, U)
         for c in range(4):
-            lo, hi = 128 * c, 128 * c + 128
-            op(v(128), lambda x, q, lo=lo, hi=hi: [x["v"].tensor_tensor(x["T"].hd[:, lo:hi], x["T"].tl[:, 384:512], x["T"].dif[:, lo:hi], A.mult)],
-               rd=[("tl", 0, 512), ("dif", lo, hi)], wr=[("hd", lo, hi)])
-        op(v(512), lambda x, q: [x["v"].tensor_tensor(x["T"].mg[:], x["T"].hp[:], x["T"].hd[:], A.add)], rd=[("hp", 0, 512), ("hd", 0, 512)], wr=[("mg", 0, 512)])
-        copy("cu%d" % d, "mg", 0, 512)
+            tt("pick %d %d" % (d, c), "xx", 128 * c, 128 * c + 128, "tl", 256, "dif", 128 * c, A.mult)
+        tt("join %d" % d, "mg", 0, 512, "xx", 0, "mid", 0, A.add)
+        ts("copy cu%d" % d, "cu%d" % d, 0, 512, "mg", 0, W / 2, None, A.add, c=0.5)
 
     copy("shown_u", "shown_i", 0, 48)
-    send(1)
+    got = send(1)
+    if cut < H:
+        load("sus1", "sus", "tab", cut, H, "Y", (H - cut) // 4, deps=got[:1])
+    load("away", "away", "away_i", 0, 512, "Y", 256, deps=[got[CFG["away_after"]]])
     copy("hu1", "c1", 0, 128)
-    for u in range(U):
-        tables(1, u)
     copy("cu1", "home_i", 0, 512)
-    copy("hp", "home_i", 0, 512)
-    op(v(512), lambda x, q: [x["v"].tensor_tensor(x["T"].dif[:], x["T"].away_i[:], x["T"].hp[:], A.subtract)], rd=[("away_i", 0, 512), ("hp", 0, 512)], wr=[("dif", 0, 512)])
+    ts("mid", "mid", 0, 512, "cu1", 0, -W / 2, None, A.add, c=0.5)
+    tables(1, 0, U)
+    tt("dif", "dif", 0, 512, "away_i", 0, "home_i", 0, A.subtract)
     for d in range(1, DAYS + 1):
-        low(d)
-        for u in range(U):
-            halves(d, u)
-        for u in range(U):
-            base(d, u)
-        for u0, u1 in GROUPS:
+        for u0, u1 in CFG["halves"]:
+            halves(d, u0, u1)
+        pieces = {}
+        for u0, u1 in CFG["spans"]:
+            got = contacts(d, u0, u1)
             for u in range(u0, u1):
-                pressure(d, u)
+                pieces[u] = got
+        for u0, u1 in CFG["groups"][d - 1]:
+            for u in range(u0, u1):
+                pressure(d, u, pieces[u])
             outcome(d, u0, u1)
-            for b0, b1 in BATCHES:
-                if b1 == u1:
+            for w0, w1 in CFG["news"][d - 1]:
+                if u0 < w1 <= u1:
+                    renew(d, w0, w1)
+            for b0, b1 in CFG["batches"][d - 1]:
+                if u0 < b1 <= u1:
                     histories(d, b0, b1)
                     if d < DAYS:
-                        for w in range(b0, b1):
-                            tables(d + 1, w)
+                        tables(d + 1, b0, b1)
         if d < DAYS:
             send(d + 1)
-            contacts(d + 1)
-    op({"Y": (1, 0, 0, 0)}, lambda x, q: [x["y"].dma_start(x["T"].h[:], x["T"].c4[:])], rd=[("c4", 0, 128)], lat=("dma", 64), token="h")
+            lists(d + 1)
+    mine = [i for i, o in enumerate(ops) if "G" in o["cost"]]
+    own = sorted((i for i in mine if ops[i]["token"] is None), key=lambda i: ops[i]["name"] == "select em")
+    calls = [i for i in mine if ops[i]["token"] is not None]
+    early, first = CFG["early"], 2 + (cut < H)
+    line = own[:early] + calls[:first] + own[early:] + calls[first:]
+    for a, b in zip(line, line[1:]):
+        ops[b]["deps"] = sorted(set(ops[b]["deps"]) | {a})
     return ops
 
 
-NOMINAL = {"V": 0.06, "S": 0.10, "P": 0.03, "G": 0.09, "Y": 0.10, "-": 0.0, "cyc": 0.00083, "gat": 1.5 * 0.00083, "pe": 0.00072,
-           "hop": 0.10, "own": 0.06, "dma": 2.0, "kb": 0.005, "remote": 2.0, "rkb": 0.008}
-SETS = [{}, {"gat": 1.1 * 0.00083, "remote": 2.5}, {"gat": 2.0 * 0.00083}, {"hop": 0.2, "own": 0.1, "pe": 0.00083, "remote": 3.0}]
-TRIES = 3000
+NOMINAL = {"V": 0.06, "S": 0.08, "P": 0.02, "G": 0.09, "Y": 0.10, "-": 0.0, "cyc": 0.00087, "gat": 1.55 * 0.00083, "pe": 0.0006,
+           "hop": 0.12, "own": 0.06, "dma": 1.2, "kb": 0.004, "row": 0.002, "remote": 1.2, "issue": 0.8, "first": 1.0}
+SETS = [{}, {"gat": 1.2 * 0.00083, "remote": 2.0, "pe": 0.00045, "kb": 0.002, "issue": 0.5}, {"gat": 2.0 * 0.00083, "cyc": 0.001, "pe": 0.0008},
+        {"hop": 0.2, "own": 0.1, "pe": 0.00083, "remote": 2.0, "dma": 2.0, "kb": 0.006, "P": 0.03, "issue": 1.2}]
 PLAN = {}
 
 
 def dur(op, q, m):
-    f, cyc, gat, pe = op["cost"][q]
-    return f * m[q] + cyc * m["cyc"] + gat * m["gat"] + pe * m["pe"]
+    c = op["cost"][q]
+    return c[0] * m[q] + c[1] * m["cyc"] + c[2] * m["gat"] + c[3] * m["pe"] + (m["issue"] if len(c) > 4 else 0.0)
 
 
-def late(op, m):
+def moved(op, m):
+    return op["lat"][1] * m["kb"] + op["lat"][2] * m["row"]
+
+
+def finish(op, t, free, m):
     if op["lat"] is None:
-        return 0.0
-    kind, kb = op["lat"]
-    return m["dma"] + kb * m["kb"] if kind == "dma" else m["remote"] + kb * m["rkb"]
+        return t
+    t += m[op["lat"][0]] / 2
+    if op["name"] == "send 1 0":
+        t += m["first"]
+    free["D"] = max(t, free["D"]) + moved(op, m)
+    return free["D"] + m[op["lat"][0]] / 2
 
 
-def schedule(ops, users, m, noise, on):
+def schedule(ops, users, m, noise, on, chain):
     n = len(ops)
     prio = [0.0] * n
     for i in range(n - 1, -1, -1):
-        prio[i] = dur(ops[i], on[i], m) + late(ops[i], m) + max([prio[j] + m["hop"] for j in users[i]] or [0.0])
+        late = 0.0 if ops[i]["lat"] is None else m[ops[i]["lat"][0]] + moved(ops[i], m)
+        prio[i] = dur(ops[i], on[i], m) + late + max([prio[j] + m["hop"] for j in users[i]] or [0.0])
     key = [prio[i] + noise[i] for i in range(n)]
     left = [len(o["deps"]) for o in ops]
-    done, free = [None] * n, {q: 0.0 for q in "VSPGY-"}
+    users = [u[:] for u in users]
+    for a, b in chain:
+        users[a].append(b)
+        left[b] += 1
+    done, free = [None] * n, {q: 0.0 for q in "VSPGY-D"}
     avail = [i for i in range(n) if left[i] == 0]
     ready, out = [None] * n, []
     while avail:
@@ -346,7 +444,7 @@ def schedule(ops, users, m, noise, on):
         for i in avail:
             q = on[i]
             if ready[i] is None:
-                ready[i] = max([done[d] + (m["own"] if on[d] == q else m["hop"]) for d in ops[i]["deps"]] or [0.0])
+                ready[i] = max([done[d] + (m["own"] if on[d] == q else m["hop"]) for d in ops[i]["needs"]] or [0.0])
             r = max(free[q], ready[i])
             if best is None or r < best[0] - 1e-9 or (r < best[0] + 1e-9 and key[i] > key[best[1]]):
                 best = (r, i)
@@ -355,7 +453,7 @@ def schedule(ops, users, m, noise, on):
         t = r + dur(ops[i], q, m)
         if q != "-":
             free[q] = t
-        done[i] = t + late(ops[i], m)
+        done[i] = finish(ops[i], t, free, m)
         out.append((r, i, q))
         avail.remove(i)
         for j in users[i]:
@@ -365,18 +463,20 @@ def schedule(ops, users, m, noise, on):
     return out
 
 
-def replay(ops, order, m):
-    done, queue, free, span = {}, {}, {q: 0.0 for q in "VSPGY-"}, 0.0
+def replay(ops, order, m, trace=None):
+    done, queue, free, span = {}, {}, {q: 0.0 for q in "VSPGY-D"}, 0.0
     for _, i, q in order:
         r = free[q] if q != "-" else 0.0
-        for d in ops[i]["deps"]:
+        for d in ops[i]["needs"]:
             t = done[d] + (m["own"] if queue[d] == q else m["hop"])
             if t > r:
                 r = t
         t = r + dur(ops[i], q, m)
         if q != "-":
             free[q] = t
-        done[i], queue[i] = t + late(ops[i], m), q
+        done[i], queue[i] = finish(ops[i], t, free, m), q
+        if trace is not None:
+            trace.append((r, t, done[i], q, ops[i]["name"]))
         span = max(span, done[i])
     return span
 
@@ -385,7 +485,7 @@ def plan():
     if PLAN:
         return PLAN
     ops = build_graph()
-    n, state = len(ops), [12345]
+    n, state = len(ops), [CFG.get("seed", 12345)]
     users = [[] for _ in range(n)]
     for i, o in enumerate(ops):
         for d in o["deps"]:
@@ -396,26 +496,75 @@ def plan():
         return (state[0] >> 8) % k
     sets = [dict(NOMINAL, **s) for s in SETS]
 
-    def judge(noise, on):
-        order = schedule(ops, users, sets[0], noise, on)
-        return sum(replay(ops, order, m) for m in sets) / len(sets), order
-    flex = [i for i in range(n) if len(ops[i]["cost"]) > 1]
-    on = ["S" if len(o["cost"]) > 1 else list(o["cost"])[0] for o in ops]
-    noise = [0.0] * n
-    best, order = judge(noise, on)
-    for _ in range(TRIES):
-        noise2, on2 = noise[:], on[:]
-        for _ in range(1 << rnd(4)):
-            if rnd(5) < 2:
-                i = flex[rnd(len(flex))]
-                on2[i] = "V" if on[i] == "S" else "S"
-            else:
-                noise2[rnd(n)] += (rnd(1001) + rnd(1001) + rnd(1001) - 1500) / 250.0
-        t, order2 = judge(noise2, on2)
-        if t <= best:
-            best, order, noise, on = t, order2, noise2, on2
-    PLAN["ops"], PLAN["order"], PLAN["time"] = ops, order, best
-    PLAN["at"] = {i: k for k, (_, i, _) in enumerate(order)}
+    on = [("S" if o["cost"]["S"][2] else list(o["cost"])[0]) if len(o["cost"]) > 1 else list(o["cost"])[0] for o in ops]
+    first = [100.0 if o["name"] == "load shown" else 0.0 for o in ops]
+    named, chain = {o["name"]: i for i, o in enumerate(ops)}, []
+    for q, names in CFG["seq"].items():
+        ids = [named[k] for k in names if k in named]
+        chain += list(zip(ids, ids[1:]))
+        for i in ids:
+            on[i] = q
+    order = [i for _, i, _ in schedule(ops, users, sets[0], first, on, chain)]
+    assert len(order) == n
+    deps = [o["needs"] for o in ops]
+    takes = [{q: [dur(o, q, m) for m in sets] for q in o["cost"]} for o in ops]
+    lat = [None if o["lat"] is None else [(m[o["lat"][0]] / 2 + (m["first"] if o["name"] == "send 1 0" else 0), moved(o, m), m[o["lat"][0]] / 2) for m in sets]
+           for o in ops]
+
+    def judge(order, on):
+        total = 0.0
+        for k, m in enumerate(sets):
+            own, hop, done, engines = m["own"], m["hop"], [0.0] * n, 0.0
+            free = {"V": 0.0, "S": 0.0, "P": 0.0, "G": 0.0, "Y": 0.0, "-": 0.0}
+            for i in order:
+                q = on[i]
+                r = free[q]
+                for d in deps[i]:
+                    t = done[d] + (own if on[d] == q else hop)
+                    if t > r:
+                        r = t
+                r += takes[i][q][k]
+                if q != "-":
+                    free[q] = r
+                if lat[i]:
+                    a, b, c = lat[i][k]
+                    engines = max(r + a, engines) + b
+                    r = engines + c
+                done[i] = r
+            total += max(done) + 0.05 * sum(done) / n
+        return total / len(sets)
+    now = judge(order, on)
+    best = (now, order, on)
+    free_ops = [i for i in range(n) if ops[i]["token"] is None]
+    for step in range(CFG["tries"]):
+        heat = CFG.get("hot", 0.15) * (0.01 / CFG.get("hot", 0.15)) ** (step / CFG["tries"])
+        i = free_ops[rnd(len(free_ops))]
+        order2, on2 = order, on
+        flip = len(takes[i]) > 1 and rnd(10) < 3
+        if flip:
+            on2 = on[:]
+            on2[i] = [q for q in takes[i] if q != on[i]][0]
+        if not flip or rnd(2):
+            at, way, q, past = order.index(i), 2 * rnd(2) - 1, on2[i], (1, 1, 1, 2, 2, 3, 5, 8)[rnd(8)]
+            along, rest, k = [i], [], at + way
+            while 0 <= k < n and past:
+                j = order[k]
+                if any(a in (ops[j]["deps"] if way > 0 else users[j]) for a in along):
+                    along.append(j)
+                else:
+                    rest.append(j)
+                    past -= on2[j] == q
+                k += way
+            if past or len(along) > 12 or any(ops[a]["token"] for a in along):
+                continue
+            order2 = order[:at] + rest + along + order[k:] if way > 0 else order[:k + 1] + along[::-1] + rest[::-1] + order[at + 1:]
+        t = judge(order2, on2)
+        if t <= now or rnd(1000000) < 1000000 * math.exp((now - t) / heat):
+            now, order, on = t, order2, on2
+            if t < best[0]:
+                best = (t, order, on)
+    PLAN["ops"], PLAN["order"], PLAN["time"] = ops, [(0, i, best[2][i]) for i in best[1]], best[0]
+    PLAN["at"] = {i: k for k, i in enumerate(best[1])}
     return PLAN
 
 
@@ -438,7 +587,7 @@ def rank_program(g, core, T, topo):
             tok[i], known[i] = (o["token"], landing), {o["token"]: landing}
             final[o["token"]] = landing
             continue
-        for d in sorted(o["deps"], key=lambda d: -p["at"][d]):
+        for d in sorted(o["needs"], key=lambda d: -p["at"][d]):
             s, n = tok[d]
             if n and seen[q].get(s, 0) < n:
                 eng[q].wait_ge(T.sem[s], n)
@@ -457,6 +606,9 @@ def rank_program(g, core, T, topo):
             final["q" + q] = count[q]
         elif o["token"] == "sent":
             tok[i] = ("sent", 0)
+        elif o["token"] == "issued":
+            tok[i] = ("issued", 1)
+            final["issued"] = 1
         else:
             calls[0].then_inc(T.sem["d_" + o["token"]], 16)
             tok[i] = ("d_" + o["token"], 16)

@@ -1,4 +1,3 @@
-import math
 from concourse.bass import DstId, RemoteDMATransfer
 from concourse.mybir import AluOpType, ActivationFunctionType
 
@@ -6,21 +5,36 @@ P, S, W, H, TH, DAYS = 2048, 256, 2816, 4096, 11008, 3
 N, U = 512, 4
 CFG = {
     "groups": [[(0, 2), (2, 3), (3, 4)]] * 3,
+    "smalls": [[(0, 3), (3, 4)]] * 2 + [[(0, 2), (2, 3), (3, 4)]],
     "news": [[(0, 2), (2, 3), (3, 4)]] * 3,
-    "batches": [[(0, 4)], [(0, 4)], [(0, 4)]],
-    "slow": [[], [], []],
-    "last_y": 0,
-    "pbank": [0, 1, 2, 0],
-    "hits": 1,
-    "spans": [(0, 1), (1, 2), (2, 3), (3, 4)],
-    "paired": set(),
-    "xbank": [3, 4, 1, 2],
-    "seq": {},
+    "batches": [[(0, 4)], [(0, 4)], [(0, 3), (3, 4)]],
     "halves": [(0, 2), (2, 4)],
-    "sus_first": 4096,
-    "away_after": 1,
-    "early": 7,
-    "tries": 80000,
+    "pbank": [0, 1, 2, 0], "xbank": [3, 4, 1, 2],
+    "hits": 4, "last_y": 256, "lifted": 2, "early": 6, "away_late": True, "calls": (2, 1),
+}
+
+DAY_V = ("con12 con13 con03 con23 con33 downsus2 score0 scan0 score2 scan2 best0 hit0 w0 wa0 wb0 %sscore3 scan3 best3 hit3 w3 wa3 wb3 new0 new2 new3 "
+         "slot1+ ha0 hb0 hc0 hd0 sus0+ pick0+ join+ cu+ downsus0+")
+DAY_S = "con10 con00 con01 con11 con02 con20 con21 con22 con30 con31 con32 downw0 downw3 half0+ slot0+ slot2+ half2+ sus1+ sus2+ sus3+"
+DAY_P = ("add10 add00 add12 add13 add01 add03 add11 add02 add20 add23 add21 add22 add33 base2 %sadd30 add31 add32 turnw0 base3 spread0 spread1 turnw3 spread2 spread3 "
+         "list00 list10 list40 list50 list60 list70 turnsus0+ base0+ turnsus1+ turnsus2+ turnsus3+ base1+")
+ORDER = {
+    "start": {
+        "V": "ones steps k0 k1 k2 k3 k4 k5 k6 k7 k8 shown k9 k10 k11 slot1+ k12 k13 k14 resets unit elev idh hd0 half0+ sus0+ cu+ sus3+ mid+ downsus0+",
+        "S": "loadshown slot0+ slot2+ half2+ sus1+ sus2+",
+        "P": "turnsus0+ turnsus1+ base0+ turnsus2+ turnsus3+ base1+",
+        "Y": "loadx loadhist loadsus loadhome loadaway",
+    },
+    "day1": {"V": DAY_V % "dif ", "S": DAY_S, "P": DAY_P % "homes "},
+    "day2": {"V": DAY_V % "", "S": DAY_S, "P": DAY_P % ""},
+    "day3": {
+        "V": "con12 con13 con02 con03 con23 downsus2 score0 scan0 best0 hit0 w0 wa0 wb0 score2 downw0 scan2 best2 w2 hit2 wa2 wb2 new0 score3 downw2 scan3 "
+             "best3 hit3 w3 wb3 wa3 new2 ha0 hb0 hc0 hd0 new3 new4 ha3 hb3 hc3 hd3",
+        "S": "con00 con01 con10 con11 con20 con21 con30 con22 con31 con33 con32 back2 lift0 downw3 storey4 storeh3",
+        "P": "add12 add00 add01 add13 add10 add02 add03 add11 add23 add21 add30 add20 add22 turnw0 add31 spread0 spread1 add33 add32 turnw2 base2 base3 spread2 "
+             "list00 list10 turnw3 spread3 list03 list13",
+        "Y": "storey0 storey2 storeh0 storey3",
+    },
 }
 
 SCRATCH = {
@@ -32,16 +46,15 @@ SCRATCH = {
     "hu1": ("sbuf", [128, 128], "uint16"), "hu2": ("sbuf", [128, 128], "uint16"), "hu3": ("sbuf", [128, 128], "uint16"),
     "home_i": ("sbuf", [128, 512], "int32"), "away_i": ("sbuf", [128, 512], "int32"), "dif": ("sbuf", [128, 512], "float32"),
     "cu1": ("sbuf", [128, 512], "uint16"), "cu2": ("sbuf", [128, 512], "uint16"), "cu3": ("sbuf", [128, 512], "uint16"),
-    "t1": ("sbuf", [128, 128], "float32"), "t2": ("sbuf", [128, 128], "int32"), "mg": ("sbuf", [128, 512], "float16"),
-    "mid": ("sbuf", [128, 512], "float16"), "ee": ("sbuf", [128, P], "bfloat16"),
+    "t1": ("sbuf", [128, 128], "float32"), "t2": ("sbuf", [128, 128], "int32"),
+    "mg": ("sbuf", [128, 512], "float16"), "mid": ("sbuf", [128, 512], "float16"), "elev": ("sbuf", [128, 512], "bfloat16"),
     "gc": ("sbuf", [128, 4 * P], "bfloat16"), "gs": ("sbuf", [128, P], "bfloat16"),
-    "g0": ("sbuf", [128, P], "float32"), "g2": ("sbuf", [128, P], "float16"),
     "st0": ("sbuf", [128, P], "bfloat16"), "st1": ("sbuf", [128, P], "bfloat16"),
     "sc": ("sbuf", [128, P], "float32"), "fs": ("sbuf", [128, P], "float32"),
     "zi": ("sbuf", [128, 32 * U], "int32"), "zz": ("sbuf", [128, 32 * U], "int32"),
     "feat": ("sbuf", [128, 128 * U], "bfloat16"), "tts": ("sbuf", [128, 128 * U], "bfloat16"),
     "h1": ("sbuf", [128, P], "bfloat16"), "h2": ("sbuf", [128, P], "bfloat16"), "h3": ("sbuf", [128, P], "bfloat16"),
-    "hr": ("sbuf", [128, P], "bfloat16"),
+    "hr": ("sbuf", [128, P], "bfloat16"), "ee": ("sbuf", [128, P], "bfloat16"),
     "snd1": ("sbuf", [128, 3 * S], "bfloat16"), "snd2": ("sbuf", [128, 3 * S], "bfloat16"), "snd3": ("sbuf", [128, 3 * S], "bfloat16"),
     "yo": ("sbuf", [128, P], "float32"),
     "ones": ("sbuf", [128, 128], "bfloat16"), "idn": ("sbuf", [128, 128], "bfloat16"), "idh": ("sbuf", [128, 128], "float16"),
@@ -50,19 +63,22 @@ SCRATCH = {
     "r4": ("sbuf", [128, 4], "float32"), "hot": ("sbuf", [128, 4], "float32"), "col": ("sbuf", [128, 8], "float32"),
     "wv": ("sbuf", [128, 128], "float32"), "wa": ("sbuf", [128, 128], "float32"), "wb": ("sbuf", [128, 128], "float32"),
     "cf": ("sbuf", [128, 128], "bfloat16"), "em": ("sbuf", [128, 512], "bfloat16"),
-    "mz": ("sbuf", [128, 128], "bfloat16"), "sel": ("sbuf", [128, 512], "bfloat16"), "lm": ("sbuf", [128, 3 * 512], "bfloat16"),
-    "xx": ("psum", [128, 2560], "float32"), "bt": ("psum", [128, 2048], "bfloat16"),
-    "tl": ("psum", [128, 512], "float32"),
+    "mz": ("sbuf", [128, 128], "bfloat16"), "sel": ("sbuf", [128, 384], "bfloat16"), "lm": ("sbuf", [128, 3 * 512], "bfloat16"),
+    "xx": ("psum", [128, 2560], "float32"), "bt": ("psum", [128, 2048], "bfloat16"), "tl": ("psum", [128, 512], "float32"),
 }
 BANKS = {n: (1024 if SCRATCH[n][2] == "bfloat16" else 512) for n in SCRATCH if SCRATCH[n][0] == "psum"}
-DMAS = ["x", "shown", "hist", "sus0", "sus1", "home", "away"] + ["y%d" % u for u in range(U + 1)] + ["h%d" % u for u in range(U)]
-SEMAPHORES = ["q" + q for q in "VSPG"] + ["d_" + n for n in DMAS] + ["arr1", "arr2", "arr3", "sent", "issued"]
+DMAS = ["x", "shown", "hist", "sus", "home", "away"] + ["y%d" % u for u in range(U + 1)] + ["h%d" % u for u in range(U)]
+SEMAPHORES = ["q" + q for q in "VSPG"] + ["d_" + n for n in DMAS] + ["arr1", "arr2", "arr3", "sent"]
 
 
 def routes(T, topo, core):
     peers = [c for c in T.cores if c != core]
     peers = [c for c in peers if topo.die(c) == topo.die(core)] + [c for c in peers if topo.die(c) != topo.die(core)]
     e = topo.engines(core, peers[0])
+    if CFG["calls"] == (3,):
+        return [[(peers[0], e[1::2]), (peers[1], e[0::4]), (peers[2], e[2::4])]]
+    if CFG["calls"] == (1, 1, 1):
+        return [[(peers[1], e)], [(peers[2], e)], [(peers[0], e)]]
     return [[(peers[0], e[0::2]), (peers[1], e[1::2])], [(peers[2], topo.engines(core, peers[2]))]]
 
 
@@ -96,28 +112,29 @@ def build_graph():
     def pe(k, n): return {"P": (k, 0, 0, k * max(64, n))}
     def gp(n): return {"G": (2, 2 * n, 0, 0)}
 
-    def load(name, src, dst, lo, hi, q, kb, deps=()):
-        op("load " + name, {q: (1, 0, 0, 0)}, lambda x, q: [x["eng"][q].dma_start(x["T"][dst][:, lo:hi], x["T"][src][:, lo:hi])], wr=[(dst, lo, hi)],
+    def load(name, dst, q, kb, deps=()):
+        n = SCRATCH[dst][1][1] if name != "x" else P
+        op(("load" + name, 0, ""), {q: (1, 0, 0, 0)}, lambda x, q: [x["eng"][q].dma_start(x["T"][dst][:, 0:n], x["T"][name][:])], wr=[(dst, 0, n)],
            lat=("dma", kb, 128), token=name, deps=deps)
 
-    cut = CFG["sus_first"]
-    load("shown", "shown", "shown_i", 0, 48, "S", 24)
-    load("x", "x", "win1", 0, P, "Y", 512)
-    load("hist", "hist", "c1", 0, 128, "S", 64)
-    load("home", "home", "home_i", 0, 512, "Y", 256)
-    if cut:
-        load("sus0", "sus", "tab", 0, cut, "Y", cut // 4)
+    load("shown", "shown_i", "S", 24)
+    load("x", "win1", "Y", 512)
+    load("hist", "c1", "Y", 64)
+    load("sus", "tab", "Y", 1024)
+    load("home", "home_i", "Y", 256)
+    if not CFG["away_late"]:
+        load("away", "away_i", "Y", 256)
 
-    def fill(buf, lo, hi, val, key=None, step=1):
-        op("fill " + buf, v((hi - lo) // step, 0.5), lambda x, q: [x["v"].memset(x["T"][buf][:, lo:hi:step], val)], wr=[(key or buf, 0 if step > 1 else lo, hi)])
+    def fill(name, buf, lo, hi, val, key=None, step=1):
+        op((name, 0, ""), v((hi - lo) // step, 0.5), lambda x, q: [x["v"].memset(x["T"][buf][:, lo:hi:step], val)], wr=[(key or buf, 0 if step > 1 else lo, hi)])
 
     def select(buf, lo, hi, src, slo, pattern, how, base, cm):
-        op("select " + buf, gp(hi - lo), lambda x, q: [x["g"].affine_select(x["T"][buf][:, lo:hi], x["T"][src][:, slo:slo + hi - lo], pattern, how, 0.0, base, cm)],
+        op(("select", 0, buf), gp(hi - lo), lambda x, q: [x["g"].affine_select(x["T"][buf][:, lo:hi], x["T"][src][:, slo:slo + hi - lo], pattern, how, 0.0, base, cm)],
            rd=[(src, slo, slo + hi - lo)], wr=[(buf, lo, hi)])
 
     def iota(buf, n, pattern, base, cm):
         kw = {} if SCRATCH[buf][2] == "int32" else {"allow_small_or_imprecise_dtypes": True}
-        op("iota " + buf, gp(n), lambda x, q: [x["g"].iota(x["T"][buf][:, 0:n], pattern, base, cm, **kw)], wr=[(buf, 0, n)])
+        op(("iota", 0, buf), gp(n), lambda x, q: [x["g"].iota(x["T"][buf][:, 0:n], pattern, base, cm, **kw)], wr=[(buf, 0, n)])
 
     def ts(name, out, lo, hi, src, slo, s1, s2, o0, o1=None, c=1.0):
         cols = [s for s in (s1, s2) if isinstance(s, tuple)]
@@ -133,41 +150,42 @@ def build_graph():
         return op(name, v(hi - lo, c), lambda x, q: [x["v"].tensor_tensor(x["T"][out][:, lo:hi], x["T"][a][:, alo:alo + hi - lo], x["T"][b][:, blo:blo + hi - lo], o)],
                   rd=[(a, alo, alo + hi - lo), (b, blo, blo + hi - lo)], wr=[(out, lo, hi)])
 
-    def copy(dst, src, lo, hi):
-        op("copy %s %d" % (dst, lo // 32), v(hi - lo), lambda x, q: [x["v"].tensor_copy(x["T"][dst][:, lo:hi], x["T"][src][:, lo:hi])], rd=[(src, lo, hi)], wr=[(dst, lo, hi)])
+    def copy(name, dst, src, lo, hi):
+        op(name, v(hi - lo), lambda x, q: [x["v"].tensor_copy(x["T"][dst][:, lo:hi], x["T"][src][:, lo:hi])], rd=[(src, lo, hi)], wr=[(dst, lo, hi)])
 
-    fill("ones", 0, 128, 1.0)
-    select("idn", 0, 128, "ones", 0, [[-1, 128]], A.is_equal, 0, 1)
-    if CFG["paired"]:
-        copy("idh", "idn", 0, 128)
+    def k(n): return ("k", 0, "%d" % n)
     wide = N * max(b - a for day in CFG["groups"] for a, b in day)
-    fill("d0", 0, wide, 1.0 / 32)
-    fill("d0", 0, wide, -1048576.0, step=16)
-    fill("feat", 3, 128 * U, 1.0, step=4, key="one")
+    fill("ones", "ones", 0, 128, 1.0)
+    select("idn", 0, 128, "ones", 0, [[-1, 128]], A.is_equal, 0, 1)
+    copy(("idh", 0, ""), "idh", "idn", 0, 128)
+    fill("steps", "d0", 0, wide, 1.0 / 32)
+    fill("resets", "d0", 0, wide, -1048576.0, step=16)
+    fill("unit", "feat", 3, 128 * U, 1.0, step=4, key="one")
+    fill("elev", "elev", 0, 512, W / 256)
     iota("pi", 1, [[1, 1]], 0, 1)
     iota("r4", 4, [[1, 4]], 0, 0)
     iota("wv", 128, [[0, 8], [-1, 16]], 15, 0)
-    ts("const", "fi", 0, 1, "pi", 0, 3, None, A.bitwise_and)
-    copy("ff", "fi", 0, 1)
-    ts("const", "hot", 0, 4, "r4", 0, ("ff", 0), None, A.is_equal)
-    ts("const", "col", 0, 1, "hot", 3, -64.0, None, A.mult)
-    ts("const", "col", 1, 2, "hot", 0, 128.0, None, A.mult)
-    ts("const", "col", 2, 3, "hot", 3, ("hot", 1), 64.0, A.subtract, A.mult)
-    ts("const", "col", 3, 4, "hot", 2, 15.0, ("hot", 3), A.mult, A.add)
-    ts("const", "col", 4, 5, "hot", 3, 16.0, ("hot", 0), A.mult, A.subtract)
-    ts("const", "col", 5, 6, "col", 4, ("hot", 2), None, A.subtract)
-    ts("const", "wa", 0, 128, "wv", 0, ("col", 0), ("col", 1), A.mult, A.add)
-    tt("const", "wb", 0, 128, "wa", 0, "wv", 0, A.mult)
-    ts("const", "cf", 0, 128, "wb", 0, ("col", 2), None, A.add)
+    ts(k(0), "fi", 0, 1, "pi", 0, 3, None, A.bitwise_and)
+    copy(k(1), "ff", "fi", 0, 1)
+    ts(k(2), "hot", 0, 4, "r4", 0, ("ff", 0), None, A.is_equal)
+    ts(k(3), "col", 0, 1, "hot", 3, -64.0, None, A.mult)
+    ts(k(4), "col", 1, 2, "hot", 0, 128.0, None, A.mult)
+    ts(k(5), "col", 2, 3, "hot", 3, ("hot", 1), 64.0, A.subtract, A.mult)
+    ts(k(6), "col", 3, 4, "hot", 2, 15.0, ("hot", 3), A.mult, A.add)
+    ts(k(7), "col", 4, 5, "hot", 3, 16.0, ("hot", 0), A.mult, A.subtract)
+    ts(k(8), "col", 5, 6, "col", 4, ("hot", 2), None, A.subtract)
+    ts(k(9), "wa", 0, 128, "wv", 0, ("col", 0), ("col", 1), A.mult, A.add)
+    tt(k(10), "wb", 0, 128, "wa", 0, "wv", 0, A.mult)
+    ts(k(11), "cf", 0, 128, "wb", 0, ("col", 2), None, A.add)
+    select("mz", 0, 128, "ones", 0, [[-4, 8], [0, 4], [-32, 4]], A.is_ge, 0, 1)
+    select("mz", 0, 128, "mz", 0, [[4, 8], [0, 4], [32, 4]], A.is_ge, 3, -1)
     for r in range(4):
         select("em", 128 * r, 128 * r + 128, "cf", 0, [[-4, 8], [0, 16]], A.is_ge, -32 * r, 1)
     select("em", 0, 512, "em", 0, [[32, 4], [4, 8], [0, 16]], A.is_ge, 3, -1)
-    select("mz", 0, 128, "ones", 0, [[-4, 8], [0, 4], [-32, 4]], A.is_ge, 0, 1)
-    select("mz", 0, 128, "mz", 0, [[4, 8], [0, 4], [32, 4]], A.is_ge, 3, -1)
-    for h in range(4):
-        select("sel", 128 * h, 128 * h + 128, "mz", 0, [[0, 8], [1, 4], [0, 4]], A.is_equal, -h, 0)
     for j, c in enumerate((("col", 3), ("col", 5), ("hot", 2))):
-        ts("const lm", "lm", 512 * j, 512 * j + 512, "sel", 0, c, None, A.mult, c=0.5)
+        ts(k(12 + j), "sel", 128 * j, 128 * j + 128, "mz", 0, c, None, A.mult, c=0.5)
+        for h in range(4):
+            select("lm", 512 * j + 128 * h, 512 * j + 128 * h + 128, "sel", 128 * j, [[0, 8], [1, 4], [0, 4]], A.is_equal, -h, 0)
 
     def gather(name, dst, lo, hi, win, whi, lst, llo, bias, lkey=None):
         k = (hi - lo) // 16
@@ -182,22 +200,23 @@ def build_graph():
         lr = (lst, llo, llo + k) if lkey is None else (lst,) + lkey
         return op(name, gat(hi - lo), emit, rd=[(win, 0, whi), lr], wr=[(dst, lo, hi)])
 
-    def move(name, dst, lo, hi, src, slo, c):
+    def move(name, dst, lo, hi, src, slo, c, bias=0.0):
         def emit(x, q):
             o, w = x["T"][dst][:, lo:hi], x["T"][src][:, slo:slo + hi - lo]
-            return [x["s"].activation(o, w, F.Copy)] if q == "S" else [x["v"].tensor_copy(o, w)]
+            if q == "S":
+                return [x["s"].activation(o, w, F.Identity, bias=bias)] if bias else [x["s"].activation(o, w, F.Copy)]
+            return [x["v"].tensor_scalar(o, w, bias, None, A.add)] if bias else [x["v"].tensor_copy(o, w)]
         op(name, vs(hi - lo, c), emit, rd=[(src, slo, slo + hi - lo)], wr=[(dst, lo, hi)])
 
     def send(d):
         win, snd, arr = "win%d" % d, "snd%d" % d, "arr%d" % d
-        got = []
         for i in range(3):
             def llo(x, i=i):
                 to = [t for call in x["routes"] for t in call][i][0]
                 return 16 * part(x["rank"], x["T"].rank_of(to))
-            got.append(gather("slot %d %d" % (d, i), snd, S * i, S * i + S, win, P, "shown_u", llo, 0.0, lkey=(0, 48)))
+            gather(("slot", d, "%d" % i), snd, S * i, S * i + S, win, P, "shown_u", llo, 0.0, lkey=(0, 48))
         calls, pos = [], 0
-        for n, size in enumerate((2, 1)):
+        for n, size in enumerate(CFG["calls"]):
             def emit(x, q, n=n, pos=pos):
                 T, trs = x["T"], []
                 for j, (to, eng) in enumerate(x["routes"][n]):
@@ -212,25 +231,20 @@ def build_graph():
                     x["g"].remote_dma_fused([RemoteDMATransfer(dst_ids=[DstId(rid=r, pnc=p)], dma_engine_mask=m, remote_sem=T.sem[arr], srcs=[a], dsts=[o])
                                              for r, p, o, a, m in trs], local_sem=T.sem["sent"])
                 return []
-            calls.append(op("send %d %d" % (d, n), {"G": (0, 0, 0, 0, 1)}, emit, rd=[(snd, S * pos, S * (pos + size))],
-                            lat=("remote", 64 * size, 128 * size), token="sent"))
+            calls.append(op(("send", d, "%d" % n), {"G": (0, 0, 0, 0, 1)}, emit, rd=[(snd, S * pos, S * (pos + size))],
+                            lat=("remote", 64 * (size + size // 3), 128 * (size + size // 3)), token="sent"))
             pos += size
-        issued = None
-        if d == 1 and cut < H:
-            issued = op("issued", {"G": (1, 0, 0, 0)}, lambda x, q: [x["g"].sem_inc(x["T"].sem["issued"], 1)], token="issued")
-        return issued, op("landed %d" % d, {"-": (0, 0, 0, 0)}, None, wr=[(win, P, W)], token=arr, deps=calls)
+        return op(("landed", d, ""), {"-": (0, 0, 0, 0)}, None, wr=[(win, P, W)], token=arr, deps=calls)
 
-    def tables(d, u0, u1):
-        st = "st%d" % (d % 2)
-        for u in range(u0, u1):
+    def tables(d):
+        for u in range(U):
             i0, e = N * u, N * u + N
-            gather("sus %d %d" % (d, u), "gs", i0, e, "tab", H, "hu%d" % d, i0 // 16, 0.0)
-            op("turn sus %d %d" % (d, u), pe(4, 128),
+            gather(("sus", d, "%d" % u), "gs", i0, e, "tab", H, "hu%d" % d, i0 // 16, 0.0)
+            op(("turnsus", d, "%d" % u), pe(4, 128),
                lambda x, q, i0=i0, e=e: [x["t"].transpose(x["T"].bt[:, i0 + 128 * k:i0 + 128 * k + 128], x["T"].gs[:, i0 + k:e:4], x["T"].idn[:]) for k in range(4)],
                rd=[("gs", i0, e), ("idn", 0, 128)], wr=[("bt", i0, e)])
-            if u % 2 or u == u1 - 1:
-                lo = max(N * u0, N * (u - u % 2))
-                move("down sus %d %d" % (d, u), st, lo, e, "bt", lo, 0.5)
+            if u % 2:
+                move(("downsus", d, "%d" % (u - 1)), "st%d" % (d % 2), i0 - N, e, "bt", i0 - N, 0.5)
 
     def halves(d, u0, u1):
         i0, e, dst, win = N * u0, N * u1, "h%d" % d, "win%d" % d
@@ -240,354 +254,186 @@ def build_graph():
         def emit(x, q):
             o, w = x["T"][to][:, i0:e], x["T"][win][:, i0:e]
             return [x["s"].activation(o, w, F.Identity, bias=add, scale=0.5)] if q == "S" else [x["v"].tensor_scalar(o, w, 0.5, add, A.mult, A.add)]
-        op("half %d %d" % (d, u0), vs(e - i0, 0.5), emit, rd=[(win, i0, e)], wr=[(to, i0, e)])
-        if d == DAYS:
-            def back(x, q):
-                o, w = x["T"][dst][:, i0:e], x["T"].hr[:, i0:e]
-                return [x["s"].activation(o, w, F.Identity, bias=255.0)] if q == "S" else [x["v"].tensor_scalar(o, w, 255.0, None, A.add)]
-            op("back %d" % u0, vs(e - i0, 0.5), back, rd=[("hr", i0, e)], wr=[(dst, i0, e)])
+        op(("half", d, "%d" % u0), vs(e - i0, 0.5), emit, rd=[(win, i0, e)], wr=[(to, i0, e)])
+        if d == DAYS and u1 > CFG["lifted"]:
+            lo = max(i0, N * CFG["lifted"])
+            move(("back", d, "%d" % u0), dst, lo, e, "hr", lo, 0.5, 255.0)
 
-    def base(d, u):
-        i0, e, hh, b = N * u, N * u + N, "h%d" % d, N * CFG["xbank"][u]
-        op("base %d %d" % (d, u), pe(1, N), lambda x, q: [x["t"].matmul(x["T"].xx[:, b:b + N], x["T"].idn[:], x["T"][hh][:, i0:e], True, False)],
-           rd=[(hh, i0, e), ("idn", 0, 128)], wr=[("xx", b, b + N)])
-
-    def contacts(d, u0, u1):
-        i0, e, win, cu = N * u0, N * u1, "win%d" % d, "cu%d" % d
-        bias = 0.0 if d == 1 else 255.0
-        mine = [c for c in range(4) if (c, u0) in CFG["paired"]]
+    def pressure(d, u):
+        i0, b = N * u, N * CFG["pbank"][u]
         for c in range(4):
-            a, name = 128 * c + i0 // 16, "con %d %d %d" % (d, u0, c)
-            if mine and c == 0:
-                gather(name, "g0", i0, e, win, W, cu, a, 2 * bias)
-            elif c in mine:
-                op(name, {"V": (1, 0, e - i0, 0)},
-                   lambda x, q, a=a: [x["v"].tensor_tensor(x["T"].g2[:, i0:e], x["T"][win][:, 0:W].indirect(x["T"][cu][:, a:a + (e - i0) // 16]), x["T"].g0[:, i0:e], A.add)],
-                   rd=[(win, 0, W), (cu, a, a + (e - i0) // 16), ("g0", i0, e)], wr=[("g2", i0, e)])
-            else:
-                gather(name, "gc", P * c + i0, P * c + e, win, W, cu, a, bias)
-        return [("g2", 0, "idh") if c in mine else ("gc", P * c, "idn") for c in range(4) if not (mine and c == 0)]
+            gather(("con", d, "%d%d" % (u, c)), "gc", P * c + i0, P * c + i0 + N, "win%d" % d, W, "cu%d" % d, 128 * c + i0 // 16, 0.0 if d == 1 else 255.0)
 
-    def pressure(d, u, pieces):
-        b, last = N * CFG["pbank"][u], len(pieces) - 1
-        for buf, at, idn in pieces:
-            def emit(x, q, buf=buf, at=at + N * u, idn=idn):
+            def emit(x, q, at=P * c + i0):
                 T, key = x["T"], (d, u)
                 t = x["open"].get(key, 0)
                 x["open"][key] = t + 1
-                return [x["t"].matmul(T.xx[:, b + 128 * k:b + 128 * k + 128], T[buf][:, at + k:at + N:4], T[idn][:], t == 0 and k == 0, t == last and k == 3) for k in range(4)]
-            op("add %d %d %d" % (d, u, at // P), pe(4, 128), emit, rd=[(buf, at + N * u, at + N * u + N), (idn, 0, 128)], wr=[("xx", b, b + N)], group=(d, u))
+                return [x["t"].matmul(T.xx[:, b + 128 * k:b + 128 * k + 128], T["gc"][:, at + k:at + N:4], T.idn[:], t == 0 and k == 0, t == 3 and k == 3) for k in range(4)]
+            op(("add", d, "%d%d" % (u, c)), pe(4, 128), emit, rd=[("gc", P * c + i0, P * c + i0 + N), ("idn", 0, 128)], wr=[("xx", b, b + N)], group=(d, u))
+
+    def scores(d, u0, u1):
+        i0, e, n, b = N * u0, N * u1, N * (u1 - u0), N * CFG["pbank"][u0]
+        tt(("score", d, "%d" % u0), "sc", i0, e, "xx", b, "st%d" % (d % 2), i0, A.mult)
+        op(("scan", d, "%d" % u0), v(n), lambda x, q: [x["v"].tensor_tensor_scan(x["T"].fs[:, i0:e], x["T"].d0[:, 0:n], x["T"].sc[:, i0:e], 0.0, A.add, A.max)],
+           rd=[("sc", i0, e), ("d0", 0, n)], wr=[("fs", i0, e)])
 
     def outcome(d, u0, u1):
-        i0, e, n, m0, m1, f0, f1 = N * u0, N * u1, N * (u1 - u0), 32 * u0, 32 * u1, 128 * u0, 128 * u1
-        st, k, b, tag = "st%d" % (d % 2), u1 - u0, N * CFG["pbank"][u0], " %d %d" % (d, u0)
-        tt("score" + tag, "sc", i0, e, "xx", b, st, i0, A.mult)
-        op("scan" + tag, v(n), lambda x, q: [x["v"].tensor_tensor_scan(x["T"].fs[:, i0:e], x["T"].d0[:, 0:n], x["T"].sc[:, i0:e], 0.0, A.add, A.max)],
-           rd=[("sc", i0, e), ("d0", 0, n)], wr=[("fs", i0, e)])
-        op("best" + tag, v(32 * k), lambda x, q: [x["v"].tensor_scalar(x["T"].zi[:, m0:m1], x["T"].fs[:, i0 + 15:e:16], 32.0, 32.0 * TH + 16, A.mult, A.max)],
+        i0, e, m0, m1, f0, f1, k, tag = N * u0, N * u1, 32 * u0, 32 * u1, 128 * u0, 128 * u1, u1 - u0, "%d" % u0
+        op(("best", d, tag), v(32 * k), lambda x, q: [x["v"].tensor_scalar(x["T"].zi[:, m0:m1], x["T"].fs[:, i0 + 15:e:16], 32.0, 32.0 * TH + 16, A.mult, A.max)],
            rd=[("fs", i0, e)], wr=[("zi", m0, m1)])
-        op("hit" + tag, v(32 * k), lambda x, q: [x["v"].tensor_scalar(x["T"].feat[:, f0 + 2:f1:4], x["T"].fs[:, i0 + 15:e:16], TH + 0.75, None, A.is_gt)],
+        op(("hit", d, tag), v(32 * k), lambda x, q: [x["v"].tensor_scalar(x["T"].feat[:, f0 + 2:f1:4], x["T"].fs[:, i0 + 15:e:16], TH + 0.75, None, A.is_gt)],
            rd=[("fs", i0, e)], wr=[("f2", f0, f1)])
-        ts("w" + tag, "zz", m0, m1, "zi", m0, 31, None, A.bitwise_and)
-        op("w1" + tag, v(32 * k), lambda x, q: [x["v"].tensor_copy(x["T"].feat[:, f0:f1:4], x["T"].zz[:, m0:m1])], rd=[("zz", m0, m1)], wr=[("f0", f0, f1)])
-        op("w2" + tag, v(32 * k, 2), lambda x, q: [x["v"].tensor_tensor(x["T"].feat[:, f0 + 1:f1:4], x["T"].zz[:, m0:m1], x["T"].zz[:, m0:m1], A.mult)],
+        ts(("w", d, tag), "zz", m0, m1, "zi", m0, 31, None, A.bitwise_and)
+        op(("wa", d, tag), v(32 * k), lambda x, q: [x["v"].tensor_copy(x["T"].feat[:, f0:f1:4], x["T"].zz[:, m0:m1])], rd=[("zz", m0, m1)], wr=[("f0", f0, f1)])
+        op(("wb", d, tag), v(32 * k, 2), lambda x, q: [x["v"].tensor_tensor(x["T"].feat[:, f0 + 1:f1:4], x["T"].zz[:, m0:m1], x["T"].zz[:, m0:m1], A.mult)],
            rd=[("zz", m0, m1)], wr=[("f1", f0, f1)])
-        op("turn w" + tag, pe(k, 128),
+        op(("turnw", d, tag), pe(k, 128),
            lambda x, q: [x["t"].transpose(x["T"].bt[:, 1024 + 128 * j:1024 + 128 * j + 128], x["T"].feat[:, f0 + 128 * j:f0 + 128 * j + 128], x["T"].idn[:]) for j in range(k)],
            rd=[("f0", f0, f1), ("f1", f0, f1), ("f2", f0, f1), ("one", 0, 128 * U), ("idn", 0, 128)], wr=[("bt", 1024, 1024 + 128 * k)])
-        move("down w" + tag, "tts", f0, f1, "bt", 1024, 0.5)
+        move(("downw", d, tag), "tts", f0, f1, "bt", 1024, 0.5)
 
     def renew(d, u0, u1):
-        i0, e, tag, b, hh = N * u0, N * u1, " %d %d" % (d, u0), N * CFG["xbank"][u0], "h%d" % d
-        slow = u0 in CFG["slow"][d - 1]
+        i0, e, b = N * u0, N * u1, N * CFG["xbank"][u0]
+        low = d == DAYS and u1 <= CFG["lifted"]
+        hh = "hr" if low else "h%d" % d
         for u in range(u0, u1):
-            j, t = N * CFG["xbank"][u], 128 * u
-            if not slow:
-                base(d, u)
-            op("spread %d %d" % (d, u), pe(4, 128),
-               lambda x, q, j=j, t=t: [x["t"].matmul(x["T"].xx[:, j + r:j + N:4], x["T"].em[:, 128 * r:128 * r + 128], x["T"].tts[:, t:t + 128], slow and r == 0, r == 3)
+            a, j, t = N * u, N * CFG["xbank"][u], 128 * u
+            op(("base", d, "%d" % u), pe(1, N), lambda x, q, a=a, j=j: [x["t"].matmul(x["T"].xx[:, j:j + N], x["T"].idn[:], x["T"][hh][:, a:a + N], True, False)],
+               rd=[(hh, a, a + N), ("idn", 0, 128)], wr=[("xx", j, j + N)])
+            op(("spread", d, "%d" % u), pe(4, 128),
+               lambda x, q, j=j, t=t: [x["t"].matmul(x["T"].xx[:, j + r:j + N:4], x["T"].em[:, 128 * r:128 * r + 128], x["T"].tts[:, t:t + 128], False, r == 3)
                                        for r in range(4)],
                rd=[("tts", t, t + 128), ("em", 0, 512)], wr=[("xx", j, j + N)])
         to = "win%d" % (d + 1) if d < DAYS else "yo"
-        if slow:
-            def cut(x, q):
-                o, w = x["T"].ee[:, i0:e], x["T"].xx[:, b:b + e - i0]
-                return [x["s"].activation(o, w, F.Relu)] if q == "S" else [x["v"].tensor_scalar(o, w, 0.0, None, A.max)]
-            op("caught" + tag, vs(e - i0), cut, rd=[("xx", b, b + e - i0)], wr=[("ee", i0, e)])
-            for u in range(u0, u1):
-                j, a = N * CFG["xbank"][u], N * u
-                op("sum %d %d" % (d, u), pe(2, N),
-                   lambda x, q, j=j, a=a: [x["t"].matmul(x["T"].xx[:, j:j + N], x["T"].idn[:], x["T"][src][:, a:a + N], src == hh, src != hh) for src in (hh, "ee")],
-                   rd=[(hh, a, a + N), ("ee", a, a + N), ("idn", 0, 128)], wr=[("xx", j, j + N)])
-            move("new" + tag, to, i0, e, "xx", b, 1.0)
-        cuts = [i0, e] if d < DAYS or u1 < U else [i0, e - CFG["last_y"], e]
+        cuts = [i0, e] if d < DAYS or u1 < U or not CFG["last_y"] else [i0, e - CFG["last_y"], e]
         for n, (lo, hi) in enumerate(zip(cuts, cuts[1:])):
-            if lo == hi:
-                continue
-            if not slow:
-                tt("new" + tag, to, lo, hi, "xx", b + lo - i0, hh, lo, A.max)
+            tag = "%d" % (u0 + n)
+            tt(("new", d, tag), "ee" if low else to, lo, hi, "xx", b + lo - i0, hh, lo, A.max)
+            if low:
+                move(("lift", d, tag), to, lo, hi, "ee", lo, 1.0, 255.0)
             if d == DAYS:
-                op("store y %d" % u0, {"YS"[n]: (1, 0, 0, 0)}, lambda x, q, lo=lo, hi=hi: [x["eng"][q].dma_start(x["T"].y[:, lo:hi], x["T"].yo[:, lo:hi])], rd=[("yo", lo, hi)],
-                   lat=("dma", (hi - lo) // 2, 128), token="y%d" % (u0 + n))
+                op(("storey", d, tag), {"Y": (1, 0, 0, 0), "S": (1, 0, 0, 0)}, lambda x, q, lo=lo, hi=hi: [x["eng"][q].dma_start(x["T"].y[:, lo:hi], x["T"].yo[:, lo:hi])],
+                   rd=[("yo", lo, hi)], lat=("dma", (hi - lo) // 2, 128), token="y" + tag)
 
-    def listed(d, j, u0, u1):
-        lo, hi = 128 * j + 32 * u0, 128 * j + 32 * u1
-        op("list %d %d %d" % (d, j, u0), pe(4, hi - lo),
-           lambda x, q: [x["t"].matmul(x["T"].tl[:, lo:hi], x["T"].lm[:, 512 * j + 128 * h:512 * j + 128 * h + 128], x["T"].tts[:, 128 * u0 + h:128 * u1:4], h == 0, h == 3)
-                         for h in range(4)], rd=[("tts", 128 * u0, 128 * u1), ("lm", 512 * j, 512 * j + 512)], wr=[("tl", lo, hi)])
+    def listed(d, j, u0, u1, to="tl", at=None):
+        at = 128 * j if at is None else at
+        lo, hi = at + 32 * u0, at + 32 * u1
+        op(("list", d, "%d%d" % (at // 128, u0)), pe(4, hi - lo),
+           lambda x, q: [x["t"].matmul(x["T"][to][:, lo:hi], x["T"].lm[:, 512 * j + 128 * h:512 * j + 128 * h + 128], x["T"].tts[:, 128 * u0 + h:128 * u1:4], h == 0, h == 3)
+                         for h in range(4)], rd=[("tts", 128 * u0, 128 * u1), ("lm", 512 * j, 512 * j + 512)], wr=[(to, lo, hi)])
 
     def histories(d, u0, u1):
-        lo, hi, tag = 32 * u0, 32 * u1, " %d %d" % (d, u0)
+        lo, hi, tag = 32 * u0, 32 * u1, "%d" % u0
         listed(d, 0, u0, u1)
         listed(d, 1, u0, u1)
-        tt("hist a" + tag, "t1", lo, hi, "tl", lo, "c%d" % d, lo, A.mult)
-        tt("hist b" + tag, "t2", lo, hi, "tl", 128 + lo, "t1", lo, A.add)
-        ts("hist c" + tag, "c%d" % (d + 1), lo, hi, "t2", lo, H - 1, None, A.bitwise_and)
-        copy("hu%d" % (d + 1) if d < DAYS else "ho", "c%d" % (d + 1), lo, hi)
+        tt(("ha", d, tag), "t1", lo, hi, "tl", lo, "c%d" % d, lo, A.mult)
+        tt(("hb", d, tag), "t2", lo, hi, "tl", 128 + lo, "t1", lo, A.add)
+        ts(("hc", d, tag), "c%d" % (d + 1), lo, hi, "t2", lo, H - 1, None, A.bitwise_and)
+        copy(("hd", d, tag), "hu%d" % (d + 1) if d < DAYS else "ho", "c%d" % (d + 1), lo, hi)
         if d == DAYS:
-            op("store h %d" % u0, {"Y": (1, 0, 0, 0), "S": (1, 0, 0, 0)}, lambda x, q: [x["eng"][q].dma_start(x["T"].h[:, lo:hi], x["T"].ho[:, lo:hi])], rd=[("ho", lo, hi)],
-               lat=("dma", (hi - lo) // 2, 128), token="h%d" % u0)
+            op(("storeh", d, tag), {"Y": (1, 0, 0, 0), "S": (1, 0, 0, 0)}, lambda x, q: [x["eng"][q].dma_start(x["T"].h[:, lo:hi], x["T"].ho[:, lo:hi])],
+               rd=[("ho", lo, hi)], lat=("dma", (hi - lo) // 2, 128), token="h%d" % u0)
 
     def lists(d):
-        listed(d - 1, 2, 0, U)
-        for c in range(4):
-            tt("pick %d %d" % (d, c), "xx", 128 * c, 128 * c + 128, "tl", 256, "dif", 128 * c, A.mult)
-        tt("join %d" % d, "mg", 0, 512, "xx", 0, "mid", 0, A.add)
-        ts("copy cu%d" % d, "cu%d" % d, 0, 512, "mg", 0, W / 2, None, A.add, c=0.5)
+        k = CFG["hits"]
+        if k == 1:
+            listed(d - 1, 2, 0, U)
+        else:
+            for r in range(k):
+                listed(d - 1, 2, 0, U, "xx", 512 + 128 * r)
+        for c in range(0, 4, k):
+            tt(("pick", d, "%d" % c), "xx", 128 * c, 128 * (c + k), *(("tl", 256) if k == 1 else ("xx", 512)), "dif", 128 * c, A.mult)
+        tt(("join", d, ""), "mg", 0, 512, "xx", 0, "mid", 0, A.add)
+        ts(("cu", d, ""), "cu%d" % d, 0, 512, "mg", 0, W / 2, None, A.add, c=0.5)
 
-    copy("shown_u", "shown_i", 0, 48)
-    got = send(1)
-    if cut < H:
-        load("sus1", "sus", "tab", cut, H, "Y", (H - cut) // 4, deps=got[:1])
-    load("away", "away", "away_i", 0, 512, "Y", 256, deps=[got[CFG["away_after"]]])
-    copy("hu1", "c1", 0, 128)
-    copy("cu1", "home_i", 0, 512)
-    ts("mid", "mid", 0, 512, "cu1", 0, -W / 2, None, A.add, c=0.5)
-    tables(1, 0, U)
-    tt("dif", "dif", 0, 512, "away_i", 0, "home_i", 0, A.subtract)
+    copy(("shown", 0, ""), "shown_u", "shown_i", 0, 48)
+    landed = send(1)
+    if CFG["away_late"]:
+        load("away", "away_i", "Y", 256, deps=[landed])
+    copy(("hd", 0, "0"), "hu1", "c1", 0, 128)
+    copy(("cu", 1, ""), "cu1", "home_i", 0, 512)
+    ts(("mid", 1, ""), "mid", 0, 512, "cu1", 0, -W / 2, None, A.add, c=0.5)
+    tables(1)
+    op(("homes", 1, ""), pe(2, 512),
+       lambda x, q: [x["t"].matmul(x["T"].tl[:, 0:512], x["T"][a][:], x["T"][b][:], a == "idh", a != "idh") for a, b in (("idh", "mid"), ("ones", "elev"))],
+       rd=[("idh", 0, 128), ("mid", 0, 512), ("ones", 0, 128), ("elev", 0, 512)], wr=[("tl", 0, 512)])
+    tt(("dif", 1, ""), "dif", 0, 512, "away_i", 0, "tl", 0, A.subtract)
     for d in range(1, DAYS + 1):
         for u0, u1 in CFG["halves"]:
             halves(d, u0, u1)
-        pieces = {}
-        for u0, u1 in CFG["spans"]:
-            got = contacts(d, u0, u1)
-            for u in range(u0, u1):
-                pieces[u] = got
         for u0, u1 in CFG["groups"][d - 1]:
             for u in range(u0, u1):
-                pressure(d, u, pieces[u])
-            outcome(d, u0, u1)
-            for w0, w1 in CFG["news"][d - 1]:
-                if u0 < w1 <= u1:
-                    renew(d, w0, w1)
-            for b0, b1 in CFG["batches"][d - 1]:
-                if u0 < b1 <= u1:
-                    histories(d, b0, b1)
-                    if d < DAYS:
-                        tables(d + 1, b0, b1)
+                pressure(d, u)
+            scores(d, u0, u1)
+            for v0, v1 in CFG["smalls"][d - 1]:
+                if v1 != u1:
+                    continue
+                outcome(d, v0, v1)
+                for w0, w1 in CFG["news"][d - 1]:
+                    if v0 < w1 <= v1:
+                        renew(d, w0, w1)
+                for b0, b1 in CFG["batches"][d - 1]:
+                    if v0 < b1 <= v1:
+                        histories(d, b0, b1)
         if d < DAYS:
+            tables(d + 1)
             send(d + 1)
             lists(d + 1)
-    mine = [i for i, o in enumerate(ops) if "G" in o["cost"]]
-    own = sorted((i for i in mine if ops[i]["token"] is None), key=lambda i: ops[i]["name"] == "select em")
-    calls = [i for i in mine if ops[i]["token"] is not None]
-    early, first = CFG["early"], 2 + (cut < H)
-    line = own[:early] + calls[:first] + own[early:] + calls[first:]
-    for a, b in zip(line, line[1:]):
-        ops[b]["deps"] = sorted(set(ops[b]["deps"]) | {a})
     return ops
 
 
-NOMINAL = {"V": 0.06, "S": 0.08, "P": 0.02, "G": 0.09, "Y": 0.10, "-": 0.0, "cyc": 0.00087, "gat": 1.55 * 0.00083, "pe": 0.0006,
-           "hop": 0.12, "own": 0.06, "dma": 1.2, "kb": 0.004, "row": 0.002, "remote": 1.2, "issue": 0.8, "first": 1.0}
-SETS = [{}, {"gat": 1.2 * 0.00083, "remote": 2.0, "pe": 0.00045, "kb": 0.002, "issue": 0.5}, {"gat": 2.0 * 0.00083, "cyc": 0.001, "pe": 0.0008},
-        {"hop": 0.2, "own": 0.1, "pe": 0.00083, "remote": 2.0, "dma": 2.0, "kb": 0.006, "P": 0.03, "issue": 1.2}]
-PLAN = {}
-
-
-def dur(op, q, m):
-    c = op["cost"][q]
-    return c[0] * m[q] + c[1] * m["cyc"] + c[2] * m["gat"] + c[3] * m["pe"] + (m["issue"] if len(c) > 4 else 0.0)
-
-
-def moved(op, m):
-    return op["lat"][1] * m["kb"] + op["lat"][2] * m["row"]
-
-
-def finish(op, t, free, m):
-    if op["lat"] is None:
-        return t
-    t += m[op["lat"][0]] / 2
-    if op["name"] == "send 1 0":
-        t += m["first"]
-    free["D"] = max(t, free["D"]) + moved(op, m)
-    return free["D"] + m[op["lat"][0]] / 2
-
-
-def schedule(ops, users, m, noise, on, chain):
-    n = len(ops)
-    prio = [0.0] * n
-    for i in range(n - 1, -1, -1):
-        late = 0.0 if ops[i]["lat"] is None else m[ops[i]["lat"][0]] + moved(ops[i], m)
-        prio[i] = dur(ops[i], on[i], m) + late + max([prio[j] + m["hop"] for j in users[i]] or [0.0])
-    key = [prio[i] + noise[i] for i in range(n)]
-    left = [len(o["deps"]) for o in ops]
-    users = [u[:] for u in users]
-    for a, b in chain:
-        users[a].append(b)
-        left[b] += 1
-    done, free = [None] * n, {q: 0.0 for q in "VSPGY-D"}
-    avail = [i for i in range(n) if left[i] == 0]
-    ready, out = [None] * n, []
-    while avail:
-        best = None
-        for i in avail:
-            q = on[i]
-            if ready[i] is None:
-                ready[i] = max([done[d] + (m["own"] if on[d] == q else m["hop"]) for d in ops[i]["needs"]] or [0.0])
-            r = max(free[q], ready[i])
-            if best is None or r < best[0] - 1e-9 or (r < best[0] + 1e-9 and key[i] > key[best[1]]):
-                best = (r, i)
-        r, i = best
-        q = on[i]
-        t = r + dur(ops[i], q, m)
-        if q != "-":
-            free[q] = t
-        done[i] = finish(ops[i], t, free, m)
-        out.append((r, i, q))
-        avail.remove(i)
-        for j in users[i]:
-            left[j] -= 1
-            if left[j] == 0:
-                avail.append(j)
-    return out
-
-
-def replay(ops, order, m, trace=None):
-    done, queue, free, span = {}, {}, {q: 0.0 for q in "VSPGY-D"}, 0.0
-    for _, i, q in order:
-        r = free[q] if q != "-" else 0.0
-        for d in ops[i]["needs"]:
-            t = done[d] + (m["own"] if queue[d] == q else m["hop"])
-            if t > r:
-                r = t
-        t = r + dur(ops[i], q, m)
-        if q != "-":
-            free[q] = t
-        done[i], queue[i] = finish(ops[i], t, free, m), q
-        if trace is not None:
-            trace.append((r, t, done[i], q, ops[i]["name"]))
-        span = max(span, done[i])
-    return span
+def queues(ops):
+    named = {o["name"]: i for i, o in enumerate(ops)}
+    line = {q: [] for q in "VSPGY-"}
+    for d, part_of_run in enumerate(("start", "day1", "day2", "day3")):
+        for q, words in ORDER[part_of_run].items():
+            for w in words.split():
+                kind = w.rstrip("+-").rstrip("0123456789")
+                line[q].append(named[(kind, d + w.count("+") - w.count("-"), w.rstrip("+-")[len(kind):])])
+    own = [i for i, o in enumerate(ops) if "G" in o["cost"] and o["token"] is None]
+    calls = [i for i, o in enumerate(ops) if o["token"] == "sent"]
+    first = len(CFG["calls"])
+    line["G"] = own[:CFG["early"]] + calls[:first] + own[CFG["early"]:] + calls[first:]
+    line["-"] = [i for i, o in enumerate(ops) if "-" in o["cost"]]
+    assert sorted(i for q in line for i in line[q]) == list(range(len(ops)))
+    return line
 
 
 def plan():
-    if PLAN:
-        return PLAN
     ops = build_graph()
-    n, state = len(ops), [CFG.get("seed", 12345)]
-    users = [[] for _ in range(n)]
-    for i, o in enumerate(ops):
-        for d in o["deps"]:
-            users[d].append(i)
-
-    def rnd(k):
-        state[0] = (1103515245 * state[0] + 12345) % 2147483648
-        return (state[0] >> 8) % k
-    sets = [dict(NOMINAL, **s) for s in SETS]
-
-    on = [("S" if o["cost"]["S"][2] else list(o["cost"])[0]) if len(o["cost"]) > 1 else list(o["cost"])[0] for o in ops]
-    first = [100.0 if o["name"] == "load shown" else 0.0 for o in ops]
-    named, chain = {o["name"]: i for i, o in enumerate(ops)}, []
-    for q, names in CFG["seq"].items():
-        ids = [named[k] for k in names if k in named]
-        chain += list(zip(ids, ids[1:]))
-        for i in ids:
-            on[i] = q
-    order = [i for _, i, _ in schedule(ops, users, sets[0], first, on, chain)]
-    assert len(order) == n
-    deps = [o["needs"] for o in ops]
-    takes = [{q: [dur(o, q, m) for m in sets] for q in o["cost"]} for o in ops]
-    lat = [None if o["lat"] is None else [(m[o["lat"][0]] / 2 + (m["first"] if o["name"] == "send 1 0" else 0), moved(o, m), m[o["lat"][0]] / 2) for m in sets]
-           for o in ops]
-
-    def judge(order, on):
-        total = 0.0
-        for k, m in enumerate(sets):
-            own, hop, done, engines = m["own"], m["hop"], [0.0] * n, 0.0
-            free = {"V": 0.0, "S": 0.0, "P": 0.0, "G": 0.0, "Y": 0.0, "-": 0.0}
-            for i in order:
-                q = on[i]
-                r = free[q]
-                for d in deps[i]:
-                    t = done[d] + (own if on[d] == q else hop)
-                    if t > r:
-                        r = t
-                r += takes[i][q][k]
-                if q != "-":
-                    free[q] = r
-                if lat[i]:
-                    a, b, c = lat[i][k]
-                    engines = max(r + a, engines) + b
-                    r = engines + c
-                done[i] = r
-            total += max(done) + 0.05 * sum(done) / n
-        return total / len(sets)
-    now = judge(order, on)
-    best = (now, order, on)
-    free_ops = [i for i in range(n) if ops[i]["token"] is None]
-    for step in range(CFG["tries"]):
-        heat = CFG.get("hot", 0.15) * (0.01 / CFG.get("hot", 0.15)) ** (step / CFG["tries"])
-        i = free_ops[rnd(len(free_ops))]
-        order2, on2 = order, on
-        flip = len(takes[i]) > 1 and rnd(10) < 3
-        if flip:
-            on2 = on[:]
-            on2[i] = [q for q in takes[i] if q != on[i]][0]
-        if not flip or rnd(2):
-            at, way, q, past = order.index(i), 2 * rnd(2) - 1, on2[i], (1, 1, 1, 2, 2, 3, 5, 8)[rnd(8)]
-            along, rest, k = [i], [], at + way
-            while 0 <= k < n and past:
-                j = order[k]
-                if any(a in (ops[j]["deps"] if way > 0 else users[j]) for a in along):
-                    along.append(j)
-                else:
-                    rest.append(j)
-                    past -= on2[j] == q
-                k += way
-            if past or len(along) > 12 or any(ops[a]["token"] for a in along):
-                continue
-            order2 = order[:at] + rest + along + order[k:] if way > 0 else order[:k + 1] + along[::-1] + rest[::-1] + order[at + 1:]
-        t = judge(order2, on2)
-        if t <= now or rnd(1000000) < 1000000 * math.exp((now - t) / heat):
-            now, order, on = t, order2, on2
-            if t < best[0]:
-                best = (t, order, on)
-    PLAN["ops"], PLAN["order"], PLAN["time"] = ops, [(0, i, best[2][i]) for i in best[1]], best[0]
-    PLAN["at"] = {i: k for k, i in enumerate(best[1])}
-    return PLAN
+    line = queues(ops)
+    order, done, at = [], set(), {q: 0 for q in line}
+    while len(order) < len(ops):
+        before = len(order)
+        for q in line:
+            while at[q] < len(line[q]) and done.issuperset(ops[line[q][at[q]]]["deps"]):
+                order.append((line[q][at[q]], q))
+                done.add(line[q][at[q]])
+                at[q] += 1
+        assert len(order) > before
+    return ops, order
 
 
 def rank_program(g, core, T, topo):
     rank = T.rank_of(core)
     if rank is None:
         return
-    p = plan()
-    ops = p["ops"]
+    ops, order = plan()
+    place = {i: k for k, (i, _) in enumerate(order)}
     eng = {"V": g.vector, "S": g.scalar, "P": g.tensor, "G": g, "Y": g.sync}
-    x = {"g": g, "v": g.vector, "s": g.scalar, "t": g.tensor, "y": g.sync, "T": T, "topo": topo, "rank": rank, "eng": eng,
+    x = {"g": g, "v": g.vector, "s": g.scalar, "t": g.tensor, "T": T, "topo": topo, "rank": rank, "eng": eng,
          "routes": routes(T, topo, core), "open": {}, "sent": [0]}
     landing = sum(len(e) for c in T.cores if c != core for call in routes(T, topo, c) for to, e in call if to == core)
     count = {q: 0 for q in eng}
     seen = {q: {} for q in eng}
     tok, known, final = {}, {}, {}
-    for _, i, q in p["order"]:
+    for i, q in order:
         o = ops[i]
         if q == "-":
             tok[i], known[i] = (o["token"], landing), {o["token"]: landing}
             final[o["token"]] = landing
             continue
-        for d in sorted(o["needs"], key=lambda d: -p["at"][d]):
+        for d in sorted(o["deps"], key=lambda d: -place[d]):
             s, n = tok[d]
             if n and seen[q].get(s, 0) < n:
                 eng[q].wait_ge(T.sem[s], n)
@@ -606,9 +452,6 @@ def rank_program(g, core, T, topo):
             final["q" + q] = count[q]
         elif o["token"] == "sent":
             tok[i] = ("sent", 0)
-        elif o["token"] == "issued":
-            tok[i] = ("issued", 1)
-            final["issued"] = 1
         else:
             calls[0].then_inc(T.sem["d_" + o["token"]], 16)
             tok[i] = ("d_" + o["token"], 16)

from concourse.bass import DstId, RemoteDMATransfer
from concourse.mybir import AluOpType, ActivationFunctionType

P, S, W, H, TH, DAYS = 2048, 256, 2816, 4096, 11008, 3
N, U = 512, 4
CFG = {
    "groups": [[(0, 2), (2, 3), (3, 4)]] * 3,
    "smalls": [[(0, 3), (3, 4)]] * 2 + [[(0, 2), (2, 3), (3, 4)]],
    "news": [[(0, 2), (2, 3), (3, 4)]] * 3,
    "batches": [[(0, 4)], [(0, 4)], [(0, 3), (3, 4)]],
    "halves": [(0, 2), (2, 4)],
    "pbank": [0, 1, 2, 0], "xbank": [3, 4, 1, 2],
    "hits": 4, "last_y": 256, "lifted": 2, "early": 6, "away_late": True, "calls": (2, 1),
}

DAY_V = ("con12 con13 con03 con23 con33 downsus2 score0 scan0 score2 scan2 best0 hit0 w0 wa0 wb0 %sscore3 scan3 best3 hit3 w3 wa3 wb3 new0 new2 new3 "
         "slot1+ ha0 hb0 hc0 hd0 sus0+ pick0+ join+ cu+ downsus0+")
DAY_S = "con10 con00 con01 con11 con02 con20 con21 con22 con30 con31 con32 downw0 downw3 half0+ slot0+ slot2+ half2+ sus1+ sus2+ sus3+"
DAY_P = ("add10 add00 add12 add13 add01 add03 add11 add02 add20 add23 add21 add22 add33 base2 %sadd30 add31 add32 turnw0 base3 spread0 spread1 turnw3 spread2 spread3 "
         "list00 list10 list40 list50 list60 list70 turnsus0+ base0+ turnsus1+ turnsus2+ turnsus3+ base1+")
ORDER = {
    "start": {
        "V": "ones steps k0 k1 k2 k3 k4 k5 k6 k7 k8 shown k9 k10 k11 slot1+ k12 k13 k14 resets unit elev idh hd0 half0+ sus0+ cu+ sus3+ mid+ downsus0+",
        "S": "loadshown slot0+ slot2+ half2+ sus1+ sus2+",
        "P": "turnsus0+ turnsus1+ base0+ turnsus2+ turnsus3+ base1+",
        "Y": "loadx loadhist loadsus loadhome loadaway",
    },
    "day1": {"V": DAY_V % "dif ", "S": DAY_S, "P": DAY_P % "homes "},
    "day2": {"V": DAY_V % "", "S": DAY_S, "P": DAY_P % ""},
    "day3": {
        "V": "con12 con13 con02 con03 con23 downsus2 score0 scan0 best0 hit0 w0 wa0 wb0 score2 downw0 scan2 best2 w2 hit2 wa2 wb2 new0 score3 downw2 scan3 "
             "best3 hit3 w3 wb3 wa3 new2 ha0 hb0 hc0 hd0 new3 new4 ha3 hb3 hc3 hd3",
        "S": "con00 con01 con10 con11 con20 con21 con30 con22 con31 con33 con32 back2 lift0 downw3 storey4 storeh3",
        "P": "add12 add00 add01 add13 add10 add02 add03 add11 add23 add21 add30 add20 add22 turnw0 add31 spread0 spread1 add33 add32 turnw2 base2 base3 spread2 "
             "list00 list10 turnw3 spread3 list03 list13",
        "Y": "storey0 storey2 storeh0 storey3",
    },
}

SCRATCH = {
    "win1": ("sbuf", [128, W], "bfloat16"), "win2": ("sbuf", [128, W], "bfloat16"), "win3": ("sbuf", [128, W], "bfloat16"),
    "tab": ("sbuf", [128, H], "bfloat16"),
    "shown_i": ("sbuf", [128, 48], "int32"), "shown_u": ("sbuf", [128, 48], "uint16"),
    "c1": ("sbuf", [128, 128], "int32"), "c2": ("sbuf", [128, 128], "int32"), "c3": ("sbuf", [128, 128], "int32"),
    "c4": ("sbuf", [128, 128], "int32"), "ho": ("sbuf", [128, 128], "float32"),
    "hu1": ("sbuf", [128, 128], "uint16"), "hu2": ("sbuf", [128, 128], "uint16"), "hu3": ("sbuf", [128, 128], "uint16"),
    "home_i": ("sbuf", [128, 512], "int32"), "away_i": ("sbuf", [128, 512], "int32"), "dif": ("sbuf", [128, 512], "float32"),
    "cu1": ("sbuf", [128, 512], "uint16"), "cu2": ("sbuf", [128, 512], "uint16"), "cu3": ("sbuf", [128, 512], "uint16"),
    "t1": ("sbuf", [128, 128], "float32"), "t2": ("sbuf", [128, 128], "int32"),
    "mg": ("sbuf", [128, 512], "float16"), "mid": ("sbuf", [128, 512], "float16"), "elev": ("sbuf", [128, 512], "bfloat16"),
    "gc": ("sbuf", [128, 4 * P], "bfloat16"), "gs": ("sbuf", [128, P], "bfloat16"),
    "st0": ("sbuf", [128, P], "bfloat16"), "st1": ("sbuf", [128, P], "bfloat16"),
    "sc": ("sbuf", [128, P], "float32"), "fs": ("sbuf", [128, P], "float32"),
    "zi": ("sbuf", [128, 32 * U], "int32"), "zz": ("sbuf", [128, 32 * U], "int32"),
    "feat": ("sbuf", [128, 128 * U], "bfloat16"), "tts": ("sbuf", [128, 128 * U], "bfloat16"),
    "h1": ("sbuf", [128, P], "bfloat16"), "h2": ("sbuf", [128, P], "bfloat16"), "h3": ("sbuf", [128, P], "bfloat16"),
    "hr": ("sbuf", [128, P], "bfloat16"), "ee": ("sbuf", [128, P], "bfloat16"),
    "snd1": ("sbuf", [128, 3 * S], "bfloat16"), "snd2": ("sbuf", [128, 3 * S], "bfloat16"), "snd3": ("sbuf", [128, 3 * S], "bfloat16"),
    "yo": ("sbuf", [128, P], "float32"),
    "ones": ("sbuf", [128, 128], "bfloat16"), "idn": ("sbuf", [128, 128], "bfloat16"), "idh": ("sbuf", [128, 128], "float16"),
    "d0": ("sbuf", [128, 2048], "bfloat16"),
    "pi": ("sbuf", [128, 1], "int32"), "fi": ("sbuf", [128, 1], "int32"), "ff": ("sbuf", [128, 1], "float32"),
    "r4": ("sbuf", [128, 4], "float32"), "hot": ("sbuf", [128, 4], "float32"), "col": ("sbuf", [128, 8], "float32"),
    "wv": ("sbuf", [128, 128], "float32"), "wa": ("sbuf", [128, 128], "float32"), "wb": ("sbuf", [128, 128], "float32"),
    "cf": ("sbuf", [128, 128], "bfloat16"), "em": ("sbuf", [128, 512], "bfloat16"),
    "mz": ("sbuf", [128, 128], "bfloat16"), "sel": ("sbuf", [128, 384], "bfloat16"), "lm": ("sbuf", [128, 3 * 512], "bfloat16"),
    "xx": ("psum", [128, 2560], "float32"), "bt": ("psum", [128, 2048], "bfloat16"), "tl": ("psum", [128, 512], "float32"),
}
BANKS = {n: (1024 if SCRATCH[n][2] == "bfloat16" else 512) for n in SCRATCH if SCRATCH[n][0] == "psum"}
DMAS = ["x", "shown", "hist", "sus", "home", "away"] + ["y%d" % u for u in range(U + 1)] + ["h%d" % u for u in range(U)]
SEMAPHORES = ["q" + q for q in "VSPG"] + ["d_" + n for n in DMAS] + ["arr1", "arr2", "arr3", "sent"]


def routes(T, topo, core):
    peers = [c for c in T.cores if c != core]
    peers = [c for c in peers if topo.die(c) == topo.die(core)] + [c for c in peers if topo.die(c) != topo.die(core)]
    e = topo.engines(core, peers[0])
    if CFG["calls"] == (3,):
        return [[(peers[0], e[1::2]), (peers[1], e[0::4]), (peers[2], e[2::4])]]
    if CFG["calls"] == (1, 1, 1):
        return [[(peers[1], e)], [(peers[2], e)], [(peers[0], e)]]
    return [[(peers[0], e[0::2]), (peers[1], e[1::2])], [(peers[2], topo.engines(core, peers[2]))]]


def part(a, b):
    return b if b < a else b - 1


def build_graph():
    ops, seen = [], {}
    A, F = AluOpType, ActivationFunctionType

    def op(name, cost, emit, rd=(), wr=(), lat=None, token=None, group=None, deps=()):
        i, dep = len(ops), set(deps)
        acc = [(r, False) for r in rd] + [(r, True) for r in wr]
        acc = [((b, lo // BANKS[b] * BANKS[b], -(-hi // BANKS[b]) * BANKS[b]), True) if b in BANKS else ((b, lo, hi), w) for (b, lo, hi), w in acc]
        for (b, lo, hi), w in acc:
            for l2, h2, j, w2, g2 in seen.get(b, ()):
                if l2 < hi and lo < h2 and (w or w2) and j != i and (group is None or g2 != group):
                    dep.add(j)
        for (b, lo, hi), w in acc:
            old = seen.setdefault(b, [])
            if w and group is None:
                old[:] = [t for t in old if not (lo <= t[0] and t[1] <= hi)]
            old.append((lo, hi, i, w, group))
        ops.append({"name": name, "cost": cost, "emit": emit, "deps": sorted(dep), "needs": sorted(dep), "lat": lat, "token": token})
        return i

    def v(n, c=1.0): return {"V": (1, max(64, n * c), 0, 0)}
    def vs(n, c=1.0): return {"V": (1, max(64, n * c), 0, 0), "S": (1, max(64, n), 0, 0)}
    def gat(n): return {"V": (1, 0, n, 0), "S": (1, 0, n, 0)}
    def pe(k, n): return {"P": (k, 0, 0, k * max(64, n))}
    def gp(n): return {"G": (2, 2 * n, 0, 0)}

    def load(name, dst, q, kb, deps=()):
        n = SCRATCH[dst][1][1] if name != "x" else P
        op(("load" + name, 0, ""), {q: (1, 0, 0, 0)}, lambda x, q: [x["eng"][q].dma_start(x["T"][dst][:, 0:n], x["T"][name][:])], wr=[(dst, 0, n)],
           lat=("dma", kb, 128), token=name, deps=deps)

    load("shown", "shown_i", "S", 24)
    load("x", "win1", "Y", 512)
    load("hist", "c1", "Y", 64)
    load("sus", "tab", "Y", 1024)
    load("home", "home_i", "Y", 256)
    if not CFG["away_late"]:
        load("away", "away_i", "Y", 256)

    def fill(name, buf, lo, hi, val, key=None, step=1):
        op((name, 0, ""), v((hi - lo) // step, 0.5), lambda x, q: [x["v"].memset(x["T"][buf][:, lo:hi:step], val)], wr=[(key or buf, 0 if step > 1 else lo, hi)])

    def select(buf, lo, hi, src, slo, pattern, how, base, cm):
        op(("select", 0, buf), gp(hi - lo), lambda x, q: [x["g"].affine_select(x["T"][buf][:, lo:hi], x["T"][src][:, slo:slo + hi - lo], pattern, how, 0.0, base, cm)],
           rd=[(src, slo, slo + hi - lo)], wr=[(buf, lo, hi)])

    def iota(buf, n, pattern, base, cm):
        kw = {} if SCRATCH[buf][2] == "int32" else {"allow_small_or_imprecise_dtypes": True}
        op(("iota", 0, buf), gp(n), lambda x, q: [x["g"].iota(x["T"][buf][:, 0:n], pattern, base, cm, **kw)], wr=[(buf, 0, n)])

    def ts(name, out, lo, hi, src, slo, s1, s2, o0, o1=None, c=1.0):
        cols = [s for s in (s1, s2) if isinstance(s, tuple)]

        def emit(x, q):
            T = x["T"]
            a, b = [T[s[0]][:, s[1]:s[1] + 1] if isinstance(s, tuple) else s for s in (s1, s2)]
            return [x["v"].tensor_scalar(T[out][:, lo:hi], T[src][:, slo:slo + hi - lo], a, b, *([o0] if o1 is None else [o0, o1]))]
        return op(name, v(hi - lo, c), emit, rd=[(src, slo, slo + hi - lo)] + [(b, j, j + 1) for b, j in cols], wr=[(out, lo, hi)])

    def tt(name, out, lo, hi, a, alo, b, blo, o):
        c = 1.0 if a in BANKS or b in BANKS else 2.0
        return op(name, v(hi - lo, c), lambda x, q: [x["v"].tensor_tensor(x["T"][out][:, lo:hi], x["T"][a][:, alo:alo + hi - lo], x["T"][b][:, blo:blo + hi - lo], o)],
                  rd=[(a, alo, alo + hi - lo), (b, blo, blo + hi - lo)], wr=[(out, lo, hi)])

    def copy(name, dst, src, lo, hi):
        op(name, v(hi - lo), lambda x, q: [x["v"].tensor_copy(x["T"][dst][:, lo:hi], x["T"][src][:, lo:hi])], rd=[(src, lo, hi)], wr=[(dst, lo, hi)])

    def k(n): return ("k", 0, "%d" % n)
    wide = N * max(b - a for day in CFG["groups"] for a, b in day)
    fill("ones", "ones", 0, 128, 1.0)
    select("idn", 0, 128, "ones", 0, [[-1, 128]], A.is_equal, 0, 1)
    copy(("idh", 0, ""), "idh", "idn", 0, 128)
    fill("steps", "d0", 0, wide, 1.0 / 32)
    fill("resets", "d0", 0, wide, -1048576.0, step=16)
    fill("unit", "feat", 3, 128 * U, 1.0, step=4, key="one")
    fill("elev", "elev", 0, 512, W / 256)
    iota("pi", 1, [[1, 1]], 0, 1)
    iota("r4", 4, [[1, 4]], 0, 0)
    iota("wv", 128, [[0, 8], [-1, 16]], 15, 0)
    ts(k(0), "fi", 0, 1, "pi", 0, 3, None, A.bitwise_and)
    copy(k(1), "ff", "fi", 0, 1)
    ts(k(2), "hot", 0, 4, "r4", 0, ("ff", 0), None, A.is_equal)
    ts(k(3), "col", 0, 1, "hot", 3, -64.0, None, A.mult)
    ts(k(4), "col", 1, 2, "hot", 0, 128.0, None, A.mult)
    ts(k(5), "col", 2, 3, "hot", 3, ("hot", 1), 64.0, A.subtract, A.mult)
    ts(k(6), "col", 3, 4, "hot", 2, 15.0, ("hot", 3), A.mult, A.add)
    ts(k(7), "col", 4, 5, "hot", 3, 16.0, ("hot", 0), A.mult, A.subtract)
    ts(k(8), "col", 5, 6, "col", 4, ("hot", 2), None, A.subtract)
    ts(k(9), "wa", 0, 128, "wv", 0, ("col", 0), ("col", 1), A.mult, A.add)
    tt(k(10), "wb", 0, 128, "wa", 0, "wv", 0, A.mult)
    ts(k(11), "cf", 0, 128, "wb", 0, ("col", 2), None, A.add)
    select("mz", 0, 128, "ones", 0, [[-4, 8], [0, 4], [-32, 4]], A.is_ge, 0, 1)
    select("mz", 0, 128, "mz", 0, [[4, 8], [0, 4], [32, 4]], A.is_ge, 3, -1)
    for r in range(4):
        select("em", 128 * r, 128 * r + 128, "cf", 0, [[-4, 8], [0, 16]], A.is_ge, -32 * r, 1)
    select("em", 0, 512, "em", 0, [[32, 4], [4, 8], [0, 16]], A.is_ge, 3, -1)
    for j, c in enumerate((("col", 3), ("col", 5), ("hot", 2))):
        ts(k(12 + j), "sel", 128 * j, 128 * j + 128, "mz", 0, c, None, A.mult, c=0.5)
        for h in range(4):
            select("lm", 512 * j + 128 * h, 512 * j + 128 * h + 128, "sel", 128 * j, [[0, 8], [1, 4], [0, 4]], A.is_equal, -h, 0)

    def gather(name, dst, lo, hi, win, whi, lst, llo, bias, lkey=None):
        k = (hi - lo) // 16

        def emit(x, q):
            T = x["T"]
            a = llo if lkey is None else llo(x)
            o, w = T[dst][:, lo:hi], T[win][:, 0:whi].indirect(T[lst][:, a:a + k])
            if q == "S":
                return [x["s"].activation(o, w, F.Identity, bias=bias)] if bias else [x["s"].activation(o, w, F.Copy)]
            return [x["v"].tensor_scalar(o, w, bias, None, A.add)] if bias else [x["v"].tensor_copy(o, w)]
        lr = (lst, llo, llo + k) if lkey is None else (lst,) + lkey
        return op(name, gat(hi - lo), emit, rd=[(win, 0, whi), lr], wr=[(dst, lo, hi)])

    def move(name, dst, lo, hi, src, slo, c, bias=0.0):
        def emit(x, q):
            o, w = x["T"][dst][:, lo:hi], x["T"][src][:, slo:slo + hi - lo]
            if q == "S":
                return [x["s"].activation(o, w, F.Identity, bias=bias)] if bias else [x["s"].activation(o, w, F.Copy)]
            return [x["v"].tensor_scalar(o, w, bias, None, A.add)] if bias else [x["v"].tensor_copy(o, w)]
        op(name, vs(hi - lo, c), emit, rd=[(src, slo, slo + hi - lo)], wr=[(dst, lo, hi)])

    def send(d):
        win, snd, arr = "win%d" % d, "snd%d" % d, "arr%d" % d
        for i in range(3):
            def llo(x, i=i):
                to = [t for call in x["routes"] for t in call][i][0]
                return 16 * part(x["rank"], x["T"].rank_of(to))
            gather(("slot", d, "%d" % i), snd, S * i, S * i + S, win, P, "shown_u", llo, 0.0, lkey=(0, 48))
        calls, pos = [], 0
        for n, size in enumerate(CFG["calls"]):
            def emit(x, q, n=n, pos=pos):
                T, trs = x["T"], []
                for j, (to, eng) in enumerate(x["routes"][n]):
                    rid, pid, _ = x["topo"].addr(to)
                    at = P + S * part(T.rank_of(to), x["rank"])
                    trs.append((rid, pid, T[win][:, at:at + S], T[snd][:, S * (pos + j):S * (pos + j) + S], sum(1 << e for e in eng)))
                    x["sent"][0] += len(eng)
                if len(trs) == 1:
                    rid, pid, o, a, m = trs[0]
                    x["g"].remote_dma(o, a, T.sem[arr], T.sem["sent"], pid, rid, m)
                else:
                    x["g"].remote_dma_fused([RemoteDMATransfer(dst_ids=[DstId(rid=r, pnc=p)], dma_engine_mask=m, remote_sem=T.sem[arr], srcs=[a], dsts=[o])
                                             for r, p, o, a, m in trs], local_sem=T.sem["sent"])
                return []
            calls.append(op(("send", d, "%d" % n), {"G": (0, 0, 0, 0, 1)}, emit, rd=[(snd, S * pos, S * (pos + size))],
                            lat=("remote", 64 * (size + size // 3), 128 * (size + size // 3)), token="sent"))
            pos += size
        return op(("landed", d, ""), {"-": (0, 0, 0, 0)}, None, wr=[(win, P, W)], token=arr, deps=calls)

    def tables(d):
        for u in range(U):
            i0, e = N * u, N * u + N
            gather(("sus", d, "%d" % u), "gs", i0, e, "tab", H, "hu%d" % d, i0 // 16, 0.0)
            op(("turnsus", d, "%d" % u), pe(4, 128),
               lambda x, q, i0=i0, e=e: [x["t"].transpose(x["T"].bt[:, i0 + 128 * k:i0 + 128 * k + 128], x["T"].gs[:, i0 + k:e:4], x["T"].idn[:]) for k in range(4)],
               rd=[("gs", i0, e), ("idn", 0, 128)], wr=[("bt", i0, e)])
            if u % 2:
                move(("downsus", d, "%d" % (u - 1)), "st%d" % (d % 2), i0 - N, e, "bt", i0 - N, 0.5)

    def halves(d, u0, u1):
        i0, e, dst, win = N * u0, N * u1, "h%d" % d, "win%d" % d
        to = dst if d < DAYS else "hr"
        add = -255.375 if d == 1 else -127.875

        def emit(x, q):
            o, w = x["T"][to][:, i0:e], x["T"][win][:, i0:e]
            return [x["s"].activation(o, w, F.Identity, bias=add, scale=0.5)] if q == "S" else [x["v"].tensor_scalar(o, w, 0.5, add, A.mult, A.add)]
        op(("half", d, "%d" % u0), vs(e - i0, 0.5), emit, rd=[(win, i0, e)], wr=[(to, i0, e)])
        if d == DAYS and u1 > CFG["lifted"]:
            lo = max(i0, N * CFG["lifted"])
            move(("back", d, "%d" % u0), dst, lo, e, "hr", lo, 0.5, 255.0)

    def pressure(d, u):
        i0, b = N * u, N * CFG["pbank"][u]
        for c in range(4):
            gather(("con", d, "%d%d" % (u, c)), "gc", P * c + i0, P * c + i0 + N, "win%d" % d, W, "cu%d" % d, 128 * c + i0 // 16, 0.0 if d == 1 else 255.0)

            def emit(x, q, at=P * c + i0):
                T, key = x["T"], (d, u)
                t = x["open"].get(key, 0)
                x["open"][key] = t + 1
                return [x["t"].matmul(T.xx[:, b + 128 * k:b + 128 * k + 128], T["gc"][:, at + k:at + N:4], T.idn[:], t == 0 and k == 0, t == 3 and k == 3) for k in range(4)]
            op(("add", d, "%d%d" % (u, c)), pe(4, 128), emit, rd=[("gc", P * c + i0, P * c + i0 + N), ("idn", 0, 128)], wr=[("xx", b, b + N)], group=(d, u))

    def scores(d, u0, u1):
        i0, e, n, b = N * u0, N * u1, N * (u1 - u0), N * CFG["pbank"][u0]
        tt(("score", d, "%d" % u0), "sc", i0, e, "xx", b, "st%d" % (d % 2), i0, A.mult)
        op(("scan", d, "%d" % u0), v(n), lambda x, q: [x["v"].tensor_tensor_scan(x["T"].fs[:, i0:e], x["T"].d0[:, 0:n], x["T"].sc[:, i0:e], 0.0, A.add, A.max)],
           rd=[("sc", i0, e), ("d0", 0, n)], wr=[("fs", i0, e)])

    def outcome(d, u0, u1):
        i0, e, m0, m1, f0, f1, k, tag = N * u0, N * u1, 32 * u0, 32 * u1, 128 * u0, 128 * u1, u1 - u0, "%d" % u0
        op(("best", d, tag), v(32 * k), lambda x, q: [x["v"].tensor_scalar(x["T"].zi[:, m0:m1], x["T"].fs[:, i0 + 15:e:16], 32.0, 32.0 * TH + 16, A.mult, A.max)],
           rd=[("fs", i0, e)], wr=[("zi", m0, m1)])
        op(("hit", d, tag), v(32 * k), lambda x, q: [x["v"].tensor_scalar(x["T"].feat[:, f0 + 2:f1:4], x["T"].fs[:, i0 + 15:e:16], TH + 0.75, None, A.is_gt)],
           rd=[("fs", i0, e)], wr=[("f2", f0, f1)])
        ts(("w", d, tag), "zz", m0, m1, "zi", m0, 31, None, A.bitwise_and)
        op(("wa", d, tag), v(32 * k), lambda x, q: [x["v"].tensor_copy(x["T"].feat[:, f0:f1:4], x["T"].zz[:, m0:m1])], rd=[("zz", m0, m1)], wr=[("f0", f0, f1)])
        op(("wb", d, tag), v(32 * k, 2), lambda x, q: [x["v"].tensor_tensor(x["T"].feat[:, f0 + 1:f1:4], x["T"].zz[:, m0:m1], x["T"].zz[:, m0:m1], A.mult)],
           rd=[("zz", m0, m1)], wr=[("f1", f0, f1)])
        op(("turnw", d, tag), pe(k, 128),
           lambda x, q: [x["t"].transpose(x["T"].bt[:, 1024 + 128 * j:1024 + 128 * j + 128], x["T"].feat[:, f0 + 128 * j:f0 + 128 * j + 128], x["T"].idn[:]) for j in range(k)],
           rd=[("f0", f0, f1), ("f1", f0, f1), ("f2", f0, f1), ("one", 0, 128 * U), ("idn", 0, 128)], wr=[("bt", 1024, 1024 + 128 * k)])
        move(("downw", d, tag), "tts", f0, f1, "bt", 1024, 0.5)

    def renew(d, u0, u1):
        i0, e, b = N * u0, N * u1, N * CFG["xbank"][u0]
        low = d == DAYS and u1 <= CFG["lifted"]
        hh = "hr" if low else "h%d" % d
        for u in range(u0, u1):
            a, j, t = N * u, N * CFG["xbank"][u], 128 * u
            op(("base", d, "%d" % u), pe(1, N), lambda x, q, a=a, j=j: [x["t"].matmul(x["T"].xx[:, j:j + N], x["T"].idn[:], x["T"][hh][:, a:a + N], True, False)],
               rd=[(hh, a, a + N), ("idn", 0, 128)], wr=[("xx", j, j + N)])
            op(("spread", d, "%d" % u), pe(4, 128),
               lambda x, q, j=j, t=t: [x["t"].matmul(x["T"].xx[:, j + r:j + N:4], x["T"].em[:, 128 * r:128 * r + 128], x["T"].tts[:, t:t + 128], False, r == 3)
                                       for r in range(4)],
               rd=[("tts", t, t + 128), ("em", 0, 512)], wr=[("xx", j, j + N)])
        to = "win%d" % (d + 1) if d < DAYS else "yo"
        cuts = [i0, e] if d < DAYS or u1 < U or not CFG["last_y"] else [i0, e - CFG["last_y"], e]
        for n, (lo, hi) in enumerate(zip(cuts, cuts[1:])):
            tag = "%d" % (u0 + n)
            tt(("new", d, tag), "ee" if low else to, lo, hi, "xx", b + lo - i0, hh, lo, A.max)
            if low:
                move(("lift", d, tag), to, lo, hi, "ee", lo, 1.0, 255.0)
            if d == DAYS:
                op(("storey", d, tag), {"Y": (1, 0, 0, 0), "S": (1, 0, 0, 0)}, lambda x, q, lo=lo, hi=hi: [x["eng"][q].dma_start(x["T"].y[:, lo:hi], x["T"].yo[:, lo:hi])],
                   rd=[("yo", lo, hi)], lat=("dma", (hi - lo) // 2, 128), token="y" + tag)

    def listed(d, j, u0, u1, to="tl", at=None):
        at = 128 * j if at is None else at
        lo, hi = at + 32 * u0, at + 32 * u1
        op(("list", d, "%d%d" % (at // 128, u0)), pe(4, hi - lo),
           lambda x, q: [x["t"].matmul(x["T"][to][:, lo:hi], x["T"].lm[:, 512 * j + 128 * h:512 * j + 128 * h + 128], x["T"].tts[:, 128 * u0 + h:128 * u1:4], h == 0, h == 3)
                         for h in range(4)], rd=[("tts", 128 * u0, 128 * u1), ("lm", 512 * j, 512 * j + 512)], wr=[(to, lo, hi)])

    def histories(d, u0, u1):
        lo, hi, tag = 32 * u0, 32 * u1, "%d" % u0
        listed(d, 0, u0, u1)
        listed(d, 1, u0, u1)
        tt(("ha", d, tag), "t1", lo, hi, "tl", lo, "c%d" % d, lo, A.mult)
        tt(("hb", d, tag), "t2", lo, hi, "tl", 128 + lo, "t1", lo, A.add)
        ts(("hc", d, tag), "c%d" % (d + 1), lo, hi, "t2", lo, H - 1, None, A.bitwise_and)
        copy(("hd", d, tag), "hu%d" % (d + 1) if d < DAYS else "ho", "c%d" % (d + 1), lo, hi)
        if d == DAYS:
            op(("storeh", d, tag), {"Y": (1, 0, 0, 0), "S": (1, 0, 0, 0)}, lambda x, q: [x["eng"][q].dma_start(x["T"].h[:, lo:hi], x["T"].ho[:, lo:hi])],
               rd=[("ho", lo, hi)], lat=("dma", (hi - lo) // 2, 128), token="h%d" % u0)

    def lists(d):
        k = CFG["hits"]
        if k == 1:
            listed(d - 1, 2, 0, U)
        else:
            for r in range(k):
                listed(d - 1, 2, 0, U, "xx", 512 + 128 * r)
        for c in range(0, 4, k):
            tt(("pick", d, "%d" % c), "xx", 128 * c, 128 * (c + k), *(("tl", 256) if k == 1 else ("xx", 512)), "dif", 128 * c, A.mult)
        tt(("join", d, ""), "mg", 0, 512, "xx", 0, "mid", 0, A.add)
        ts(("cu", d, ""), "cu%d" % d, 0, 512, "mg", 0, W / 2, None, A.add, c=0.5)

    copy(("shown", 0, ""), "shown_u", "shown_i", 0, 48)
    landed = send(1)
    if CFG["away_late"]:
        load("away", "away_i", "Y", 256, deps=[landed])
    copy(("hd", 0, "0"), "hu1", "c1", 0, 128)
    copy(("cu", 1, ""), "cu1", "home_i", 0, 512)
    ts(("mid", 1, ""), "mid", 0, 512, "cu1", 0, -W / 2, None, A.add, c=0.5)
    tables(1)
    op(("homes", 1, ""), pe(2, 512),
       lambda x, q: [x["t"].matmul(x["T"].tl[:, 0:512], x["T"][a][:], x["T"][b][:], a == "idh", a != "idh") for a, b in (("idh", "mid"), ("ones", "elev"))],
       rd=[("idh", 0, 128), ("mid", 0, 512), ("ones", 0, 128), ("elev", 0, 512)], wr=[("tl", 0, 512)])
    tt(("dif", 1, ""), "dif", 0, 512, "away_i", 0, "tl", 0, A.subtract)
    for d in range(1, DAYS + 1):
        for u0, u1 in CFG["halves"]:
            halves(d, u0, u1)
        for u0, u1 in CFG["groups"][d - 1]:
            for u in range(u0, u1):
                pressure(d, u)
            scores(d, u0, u1)
            for v0, v1 in CFG["smalls"][d - 1]:
                if v1 != u1:
                    continue
                outcome(d, v0, v1)
                for w0, w1 in CFG["news"][d - 1]:
                    if v0 < w1 <= v1:
                        renew(d, w0, w1)
                for b0, b1 in CFG["batches"][d - 1]:
                    if v0 < b1 <= v1:
                        histories(d, b0, b1)
        if d < DAYS:
            tables(d + 1)
            send(d + 1)
            lists(d + 1)
    return ops


def queues(ops):
    named = {o["name"]: i for i, o in enumerate(ops)}
    line = {q: [] for q in "VSPGY-"}
    for d, part_of_run in enumerate(("start", "day1", "day2", "day3")):
        for q, words in ORDER[part_of_run].items():
            for w in words.split():
                kind = w.rstrip("+-").rstrip("0123456789")
                line[q].append(named[(kind, d + w.count("+") - w.count("-"), w.rstrip("+-")[len(kind):])])
    own = [i for i, o in enumerate(ops) if "G" in o["cost"] and o["token"] is None]
    calls = [i for i, o in enumerate(ops) if o["token"] == "sent"]
    first = len(CFG["calls"])
    line["G"] = own[:CFG["early"]] + calls[:first] + own[CFG["early"]:] + calls[first:]
    line["-"] = [i for i, o in enumerate(ops) if "-" in o["cost"]]
    assert sorted(i for q in line for i in line[q]) == list(range(len(ops)))
    return line


def plan():
    ops = build_graph()
    line = queues(ops)
    order, done, at = [], set(), {q: 0 for q in line}
    while len(order) < len(ops):
        before = len(order)
        for q in line:
            while at[q] < len(line[q]) and done.issuperset(ops[line[q][at[q]]]["deps"]):
                order.append((line[q][at[q]], q))
                done.add(line[q][at[q]])
                at[q] += 1
        assert len(order) > before
    return ops, order


def rank_program(g, core, T, topo):
    rank = T.rank_of(core)
    if rank is None:
        return
    ops, order = plan()
    place = {i: k for k, (i, _) in enumerate(order)}
    eng = {"V": g.vector, "S": g.scalar, "P": g.tensor, "G": g, "Y": g.sync}
    x = {"g": g, "v": g.vector, "s": g.scalar, "t": g.tensor, "T": T, "topo": topo, "rank": rank, "eng": eng,
         "routes": routes(T, topo, core), "open": {}, "sent": [0]}
    landing = sum(len(e) for c in T.cores if c != core for call in routes(T, topo, c) for to, e in call if to == core)
    count = {q: 0 for q in eng}
    seen = {q: {} for q in eng}
    tok, known, final = {}, {}, {}
    for i, q in order:
        o = ops[i]
        if q == "-":
            tok[i], known[i] = (o["token"], landing), {o["token"]: landing}
            final[o["token"]] = landing
            continue
        for d in sorted(o["deps"], key=lambda d: -place[d]):
            s, n = tok[d]
            if n and seen[q].get(s, 0) < n:
                eng[q].wait_ge(T.sem[s], n)
                for s2, n2 in known[d].items():
                    if seen[q].get(s2, 0) < n2:
                        seen[q][s2] = n2
        if q == "G" and o["token"] is None and seen["G"].get("qG", 0) < count["G"]:
            g.wait_ge(T.sem["qG"], count["G"])
            seen["G"]["qG"] = count["G"]
        calls = o["emit"](x, q)
        if o["token"] is None:
            for c in calls:
                count[q] += 1
                c.then_inc(T.sem["q" + q], 1)
            tok[i] = ("q" + q, count[q])
            final["q" + q] = count[q]
        elif o["token"] == "sent":
            tok[i] = ("sent", 0)
        else:
            calls[0].then_inc(T.sem["d_" + o["token"]], 16)
            tok[i] = ("d_" + o["token"], 16)
            final["d_" + o["token"]] = 16
        known[i] = dict(seen[q])
        known[i][tok[i][0]] = max(known[i].get(tok[i][0], 0), tok[i][1])
    final["sent"] = x["sent"][0]
    for s in sorted(final):
        if final[s] and seen["G"].get(s, 0) < final[s]:
            g.wait_ge(T.sem[s], final[s])
